import numpy as np, ml_dtypes
CORES = [2,6,10,14,18,22,26,30]
N = 8
BF = ml_dtypes.bfloat16
def f(rng, *shape):
    return (rng.standard_normal(shape, dtype=np.float32) * np.exp2(rng.integers(-2, 3, shape[:-1] + (1,)))).astype(BF)
def wide(rng, *shape):
    v = f(rng, *shape).astype(np.float32); k = shape[:-2] + (1, shape[-1])
    return (v * np.exp2(rng.integers(-6, 7, k)) * (rng.random(k) > 0.0625)).astype(BF)
def gentries(a):
    return np.ascontiguousarray(a.reshape(8, 16, -1).transpose(0, 2, 1)).reshape(8, -1)
def gtable(e):
    e = np.asarray(e); return np.ascontiguousarray(e.reshape(8, -1, 16).transpose(0, 2, 1)).reshape(128, -1).astype(np.int32)
WAY = "abcd"; W = len(WAY)
IC, CG, CAPP, TOT, S = 2048, 256, 256, 2048, 512
def numbers(a):
    return np.stack([gentries(u) for u in a])
def slots(a):
    return np.stack([gentries(u) for u in a]).reshape(N, N, CAPP)
def columns(t, a):
    e = slots(a); t = t.astype(np.float64)
    return np.stack([np.concatenate([t[q][:, e[q, r]] for q in range(N)], axis=1) for r in range(N)])
def sums(t, x):
    return np.stack([np.bincount(x, weights=t[o], minlength=TOT) for o in range(16)])
def home(p, a):
    e = slots(a); y = np.zeros((N, 16, IC), np.float64)
    for q in range(N):
        for r in range(N):
            y[q][:, e[q, r]] += p[r][:, q * CAPP:(q + 1) * CAPP]
    return y
def anyslots(rng):
    return np.argsort(rng.random((W, N, N, IC)), axis=-1)[..., :CAPP]
def anynumbers(rng):
    x = rng.integers(0, TOT, (W, N, 8, S)); few = rng.integers(0, TOT, (W, N, 8, 32))
    return np.where(rng.random(x.shape) < 0.5, np.take_along_axis(few, rng.integers(0, 32, x.shape), axis=-1), x)
def make(rng, x, e):
    o = np.argsort(x[0], axis=-1, kind="stable"); x = np.stack([np.take_along_axis(u, o, axis=-1) for u in x])
    ob = np.lexsort((rng.random(x[1].shape), x[1]), axis=-1)
    d = {"f" + c: f(rng, N, 16, IC) for c in WAY}
    d["v"] = (rng.standard_normal((N, 8, S)) * np.exp2(rng.integers(-1, 2, (N, 8, 1)))).astype(np.float32)
    for w, c in enumerate(WAY): d["x" + c] = np.stack([gtable(u) for u in x[w]])
    d["ob"] = np.stack([gtable(u) for u in ob])
    for w, c in enumerate(WAY): d["l" + c] = np.stack([gtable(u.reshape(8, CG)) for u in e[w]])
    return d
def setup_inputs(rng):
    return make(rng, anynumbers(rng), anyslots(rng))
def setup_inputs_runs(rng):
    x = anynumbers(rng); h = rng.integers(0, TOT, (W, N, 8, 1))
    for w in range(W): x[w, :, :, w * S // 8:w * S // 8 + S // 2] = h[w]
    x[0, :, 0:2] = h[0, :, 0:1]; x[1, :, 1:3] = h[1, :, 1:2]
    return make(rng, x, anyslots(rng))
def setup_inputs_apart(rng):
    x = np.argsort(rng.random((W, N, 8 * S // TOT, TOT)), axis=-1).reshape(W, N, 8, S)
    return make(rng, x, anyslots(rng))
def setup_inputs_ends(rng):
    x = rng.integers(0, N, (W, N, 8, S)) * CAPP + rng.integers(0, 2, (W, N, 8, S)) * (CAPP - 1)
    x = np.where(rng.random(x.shape) < 0.75, x, rng.integers(0, TOT, x.shape)); x[..., 0] = 0; x[..., 1] = TOT - 1
    e = 1 + np.argsort(rng.random((W, N, N, IC - 2)), axis=-1)[..., :CAPP]; e[..., 0] = IC - 1; e[..., -1] = 0
    return make(rng, x, e)
def setup_inputs_alike(rng):
    x = anynumbers(rng); x[:, :, 1:] = x[:, :, :1].copy()
    e = np.repeat(np.argsort(rng.random((W, N, 1, IC)), axis=-1)[..., :CAPP], N, axis=2)
    return make(rng, x, e)
def setup_inputs_spread(rng):
    d = setup_inputs(rng)
    for c in WAY[1:]: d["f" + c] = wide(rng, N, 16, IC)
    return d
def check_inputs(d):
    bad = []
    for c in WAY:
        x = numbers(d["x" + c]); e = slots(d["l" + c])
        if not np.isfinite(d["f" + c].astype(np.float32)).all(): bad.append("finite_f" + c)
        if x.min() < 0 or x.max() >= TOT: bad.append("range_x" + c)
        if e.min() < 0 or e.max() >= IC: bad.append("range_l" + c)
        if (np.diff(np.sort(e, axis=-1), axis=-1) == 0).any(): bad.append("different_l" + c)
    if not np.isfinite(d["v"]).all(): bad.append("finite_v")
    if (np.diff(numbers(d["xa"]), axis=-1) < 0).any(): bad.append("sorted_xa")
    o = numbers(d["ob"])
    if not (np.sort(o, axis=-1) == np.arange(S)).all(): bad.append("places_ob")
    elif (np.diff(np.take_along_axis(numbers(d["xb"]), o, axis=-1), axis=-1) < 0).any(): bad.append("sorted_xb_by_ob")
    return bad
def reference(fa, fb, fc, fd, v, xa, xb, xc, xd, ob, la, lb, lc, ld):
    xi = numbers(xa).reshape(N, 8 * S); xj = numbers(xb).reshape(N, 8 * S)
    w = np.repeat(v.astype(np.float64).reshape(N, 1, 8 * S), 16, axis=1)
    for t, x, a in ((fc, xc, lc), (fd, xd, ld),):
        u = columns(t, a); x = numbers(x).reshape(N, 8 * S)
        w = w * np.stack([u[r][:, x[r]] for r in range(N)])
    u = columns(fb, lb)
    ya = fa.astype(np.float64) * home([sums(w[r] * u[r][:, xj[r]], xi[r]) for r in range(N)], la)
    u = columns(ya, la)
    yb = home([sums(w[r] * u[r][:, xi[r]], xj[r]) for r in range(N)], lb)
    return {"ya": ya.astype(np.float32), "yb": yb.astype(np.float32)}

@@ -1,0 +1,325 @@
+from concourse.bass import DstId, RemoteDMATransfer
+from concourse.mybir import AluOpType as OP, ActivationFunctionType as AF
+
+F, B, I, U = "float32", "bfloat16", "int32", "uint16"
+SCRATCH = {
+    "din": ("sbuf", [128, 2048], B), "frc": ("sbuf", [128, 2048], B), "frd": ("sbuf", [128, 2048], B),
+    "frb": ("sbuf", [128, 2048], B), "fra": ("sbuf", [128, 2048], B),
+    "lt": ("sbuf", [128, 64], I), "lu": ("sbuf", [128, 64], U),
+    "xt": ("sbuf", [128, 128], I), "xr": ("sbuf", [128, 128], I), "xh": ("sbuf", [128, 128], I),
+    "xo": ("sbuf", [128, 128], I), "xu": ("sbuf", [128, 128], U),
+    "obt": ("sbuf", [128, 32], I), "obu": ("sbuf", [128, 32], U),
+    "vin": ("sbuf", [128, 512], F), "vr": ("sbuf", [128, 512], F),
+    "pc": ("sbuf", [128, 8], I), "dj": ("sbuf", [128, 512], I), "gm": ("sbuf", [128, 128], I), "jt": ("sbuf", [128, 32], I),
+    "pi": ("sbuf", [128, 8], I), "pg": ("sbuf", [128, 8], I), "col": ("sbuf", [128, 8], F),
+    "di": ("sbuf", [128, 512], I), "dk": ("sbuf", [128, 256], I), "d16": ("sbuf", [128, 512], F),
+    "eb": ("sbuf", [128, 128], B), "i2f": ("sbuf", [128, 256], F), "i2b": ("sbuf", [128, 256], B),
+    "sh1": ("sbuf", [128, 128], F), "sh2": ("sbuf", [128, 128], F), "b8": ("sbuf", [128, 128], F),
+    "gf": ("sbuf", [128, 128], F), "jf": ("sbuf", [128, 32], F),
+    "xf": ("sbuf", [128, 66], F), "y1": ("sbuf", [128, 1056], F), "fla": ("sbuf", [128, 512], F),
+    "flb": ("sbuf", [128, 512], F), "fbp": ("sbuf", [128, 512], F),
+    "ma": ("sbuf", [128, 512], F), "mb": ("sbuf", [128, 512], F),
+    "sa1": ("sbuf", [128, 32], F), "sa2": ("sbuf", [128, 32], F), "sau": ("sbuf", [128, 32], U), "sbu": ("sbuf", [128, 32], U),
+    "ba": ("sbuf", [128, 1024], F), "t1": ("sbuf", [128, 512], F), "t2": ("sbuf", [128, 256], F),
+    "t3": ("sbuf", [128, 128], F), "t4": ("sbuf", [128, 64], F), "xg": ("sbuf", [128, 40], F),
+    "ai": ("sbuf", [128, 32], I), "aj": ("sbuf", [128, 32], I), "au": ("sbuf", [128, 32], U),
+    "gcd": ("sbuf", [128, 512], B), "gb": ("sbuf", [128, 256], B),
+    "sndcd": ("dram", [1024, 64], B), "landcd": ("dram", [1024, 64], B),
+    "sndb": ("dram", [1024, 32], B), "landb": ("dram", [1024, 32], B),
+    "tcd": ("sbuf", [128, 4096], B), "tb": ("sbuf", [128, 2048], B), "ta": ("sbuf", [128, 2048], F),
+    "w1": ("sbuf", [128, 512], F), "w2": ("sbuf", [128, 512], F), "wp": ("sbuf", [128, 512], F),
+    "pr1": ("sbuf", [128, 512], F), "pr2": ("sbuf", [128, 512], F), "sg1": ("sbuf", [128, 512], F), "sg2": ("sbuf", [128, 512], F),
+    "P1": ("sbuf", [128, 2560], F), "P2": ("sbuf", [128, 2560], F), "Z1": ("sbuf", [128, 2048], F), "Z2": ("sbuf", [128, 2048], F),
+    "u1": ("sbuf", [128, 256], F), "u2": ("sbuf", [128, 256], F), "u3": ("sbuf", [128, 256], F),
+    "r1": ("sbuf", [128, 256], F), "r2": ("sbuf", [128, 256], F), "r3": ("sbuf", [128, 256], F),
+    "sndp1": ("dram", [1024, 32], F), "landp1": ("dram", [1024, 32], F), "lp1": ("sbuf", [128, 256], F),
+    "snda": ("dram", [1024, 32], F), "landa": ("dram", [1024, 32], F),
+    "sndp2": ("dram", [1024, 32], F), "landp2": ("dram", [1024, 32], F), "lp2": ("sbuf", [128, 256], F),
+    "yar": ("sbuf", [128, 2048], F), "ga": ("sbuf", [128, 256], F),
+    "ps0": ("psum", [128, 512], F), "ps1": ("psum", [128, 512], F), "ps2": ("psum", [128, 512], F), "ps3": ("psum", [128, 512], F),
+    "ps4": ("psum", [128, 512], F), "ps5": ("psum", [128, 512], F), "ps6": ("psum", [128, 512], F), "ps7": ("psum", [128, 512], F),
+}
+EXCH = ["cd", "b", "p1", "a", "p2"]
+SEMAPHORES = (["c_g", "c_v", "c_s", "c_p", "ldd", "ldl1", "ldl2", "ldc", "ldb", "lda", "ldx", "ldo", "ldv", "oya", "oyb",
+               "lp1s", "lp2s"] + [k + x for x in EXCH for k in ("snd", "self", "arr", "loc")]
+              + [k + x for x in ("cd", "b", "a") for k in ("cmp", "rot")])
+
+
+def send_engines(src, cores, topo):
+    off = [d for d in cores if topo.chip(d) != topo.chip(src)]
+    on = [d for d in cores if d != src and topo.chip(d) == topo.chip(src)]
+    e = topo.engines(src, off[0])
+    far = [d for d in off if not topo.mates(topo.chip(src), topo.chip(d)) and not topo.same_plane(topo.chip(src), topo.chip(d))]
+    near = [d for d in off if d not in far]
+    one, two = e[0::2], e[1::2]
+    n = len(two) // len(far)
+    p = {d: [one[i]] for i, d in enumerate(near)}
+    p.update({d: two[i * n:(i + 1) * n] for i, d in enumerate(far)})
+    for d in on:
+        p[d] = [x for x in topo.engines(src, d) if x not in e][0:4:2]
+    return p
+
+
+def rank_program(g, core, T, topo):
+    me = T.rank_of(core)
+    if me is None:
+        return
+    cores = list(T.cores)
+    eng = {"g": g, "v": g.vector, "s": g.scalar, "p": g.tensor, "y": g.sync}
+    seen = {q: {} for q in eng}
+    cnt, WR, RD = {}, {}, {}
+
+    def need(q, toks):
+        m = {}
+        for s, n in toks:
+            n = cnt[s] if n is None else n
+            m[s] = max(m.get(s, 0), n)
+        for s in m:
+            if seen[q].get(s, 0) < m[s]:
+                eng[q].wait_ge(T.sem[s], m[s])
+                seen[q][s] = m[s]
+
+    def before(q, rd, wr, own=None):
+        own = own or q
+        toks = []
+        for k in rd:
+            toks += [t for _, t in WR.get(k, [])]
+        for k in wr:
+            toks += [t for o, t in WR.get(k, []) + RD.get(k, []) if o != own]
+        need(q, toks)
+
+    def after(o, tok, rd, wr):
+        for k in rd:
+            RD.setdefault(k, []).append((o, tok))
+        for k in wr:
+            WR.setdefault(k, []).append((o, tok))
+
+    def run(q, fn, rd, wr, *a, **k):
+        before(q, rd, wr)
+        s = "c_" + q
+        cnt[s] = cnt.get(s, 0) + 1
+        fn(*a, **k).then_inc(T.sem[s], 1)
+        after(q, (s, cnt[s]), rd, wr)
+
+    def dma(q, sem, rd, wr, out, in_):
+        before(q, rd, wr, "d" + sem)
+        cnt[sem] = cnt.get(sem, 0) + 16
+        eng[q].dma_start(out, in_).then_inc(T.sem[sem], 16)
+        after("d" + sem, (sem, None), rd, wr)
+
+    V, S, P = g.vector, g.scalar, g.tensor
+
+    def ts(rd, wr, out, in0, s1, op0, s2=None, op1=None):
+        if op1 is None:
+            run("v", V.tensor_scalar, rd, wr, out, in0, s1, None, op0)
+        else:
+            run("v", V.tensor_scalar, rd, wr, out, in0, s1, s2, op0, op1)
+
+    def tt(rd, wr, out, a, b, op):
+        run("v", V.tensor_tensor, rd, wr, out, a, b, op)
+
+    def vcopy(rd, wr, out, in_):
+        run("v", V.tensor_copy, rd, wr, out, in_)
+
+    def scopy(rd, wr, out, in_):
+        run("s", S.activation, rd, wr, out, in_, AF.Copy)
+
+    def mm(rd, wr, out, lhsT, rhs):
+        run("p", P.matmul, rd, wr, out, lhsT, rhs, True, True)
+
+    def bank(i):
+        return T["ps%d" % i]
+
+    dma("y", "ldd", [], ["din"], T.din[0:16, :], T.fd[:, :])
+    dma("y", "ldl1", [], ["lt1"], T.lt[:, 0:16], T.lc[:, :])
+    dma("y", "ldl1", [], ["lt1"], T.lt[:, 16:32], T.ld[:, :])
+    for k in range(8):
+        dma("s" if k % 2 else "y", "ldc", [], ["frc"], T.frc[16 * k:16 * k + 16, :], T.fc[:, :])
+    dma("s", "ldl2", [], ["lt2"], T.lt[:, 32:48], T.lb[:, :])
+    dma("y", "ldl2", [], ["lt2"], T.lt[:, 48:64], T.la[:, :])
+    for k in range(8):
+        dma("s" if k % 2 else "y", "ldb", [], ["frb"], T.frb[16 * k:16 * k + 16, :], T.fb[:, :])
+    dma("y", "ldv", [], ["vin"], T.vin[0:8, :], T.v[:, :])
+    for k, x in enumerate((T.xa, T.xb, T.xc, T.xd)):
+        dma("s" if k % 2 else "y", "ldx", [], ["xt"], T.xt[:, 32 * k:32 * k + 32], x[:, :])
+    dma("y", "ldo", [], ["obt"], T.obt[:, :], T.ob[:, :])
+
+    run("g", g.iota, [], ["dj"], T.dj[:, :], [[1, 512]], 128, -1)
+    run("g", g.iota, [], ["pc"], T.pc[:, 0:1], [[1, 1]], 0, 1)
+    run("g", g.iota, [], ["gm"], T.gm[:, :], [[1, 8], [0, 16]], 0, 0)
+    run("g", g.iota, [], ["jt"], T.jt[:, :], [[16, 32]], 2048, 1)
+
+    ts(["dj"], ["di"], T.di[:, :], T.dj[:, :], 15, OP.bitwise_and)
+    ts(["di"], ["eb"], T.eb[:, :], T.di[:, 0:128], 0.0, OP.is_equal)
+    vcopy(["lt1"], ["lu1"], T.lu[:, 0:32], T.lt[:, 0:32])
+    for k in range(4):
+        mm(["eb", "din"], ["ps%d" % k], bank(k)[:, :], T.eb[0:16, :], T.din[0:16, 512 * k:512 * k + 512])
+        (scopy if k % 2 == 0 else vcopy)(["ps%d" % k], ["frd%d" % k], T.frd[:, 512 * k:512 * k + 512], bank(k)[:, :])
+    scopy(["frd%d" % k for k in range(4)] + ["lu1"], ["gcdD"], T.gcd[:, 256:512], T.frd[:, :].indirect(T.lu[:, 16:32]))
+    vcopy(["frc", "lu1"], ["gcdC"], T.gcd[:, 0:256], T.frc[:, :].indirect(T.lu[:, 0:16]))
+
+    plans = {c: send_engines(c, cores, topo) for c in cores}
+
+    def exchange(x, src, keys):
+        snd, land = T["snd" + x], T["land" + x]
+        dma("y", "snd" + x, keys, ["snd" + x], snd[:, :], src[:, :])
+        dma("y", "self" + x, keys, ["land" + x], land[128 * me:128 * me + 128, :], src[16 * me:16 * me + 16, :])
+        before("g", ["snd" + x], [])
+        tr = []
+        for d, es in plans[core].items():
+            r = cores.index(d)
+            rid, pid, _ = topo.addr(d)
+            mask = 0
+            for e in es:
+                mask |= 1 << e
+            tr.append(RemoteDMATransfer(dst_ids=[DstId(rid=rid, pnc=pid)], dma_engine_mask=mask, remote_sem=T.sem["arr" + x],
+                                        src=snd[128 * r:128 * r + 128, :], dst=land[128 * me:128 * me + 128, :]))
+        g.remote_dma_fused(tr, local_sem=T.sem["loc" + x])
+        cnt["loc" + x] = sum(len(es) for es in plans[core].values())
+        cnt["arr" + x] = sum(len(plans[c][core]) for c in cores if c != core)
+        after("remote", ("arr" + x, None), [], ["land" + x])
+
+    exchange("cd", T.gcd, ["gcdC", "gcdD"])
+    vcopy(["lt2"], ["lu2"], T.lu[:, 32:64], T.lt[:, 32:64])
+    vcopy(["frb", "lu2"], ["gb"], T.gb[:, :], T.frb[:, :].indirect(T.lu[:, 32:48]))
+    exchange("b", T.gb, ["gb"])
+    for z in ("Z1", "P2"):
+        run("g", g.iota, [], [z], T[z][:, 0:2048], [[0, 2048]], 0, 0, allow_small_or_imprecise_dtypes=True)
+
+    ts(["pc"], ["pi"], T.pi[:, 0:1], T.pc[:, 0:1], 15, OP.bitwise_and)
+    ts(["pc"], ["pg"], T.pg[:, 0:1], T.pc[:, 0:1], 4, OP.logical_shift_right)
+    ts(["pi"], ["nz"], T.col[:, 0:1], T.pi[:, 0:1], 0.0, OP.not_equal)
+    ts(["pi"], ["zf"], T.col[:, 1:2], T.pi[:, 0:1], 0.0, OP.is_equal)
+    vcopy(["pg"], ["pgf"], T.col[:, 2:3], T.pg[:, 0:1])
+    vcopy(["pc"], ["pf"], T.col[:, 3:4], T.pc[:, 0:1])
+    ts(["pg"], ["g16"], T.col[:, 4:5], T.pg[:, 0:1], 16.0, OP.mult)
+    ts(["pg"], ["rc"], T.col[:, 5:6], T.pg[:, 0:1], -256.0, OP.mult, 2048.0, OP.add)
+    ts(["di"], ["d16"], T.d16[:, :], T.di[:, :], 0.0, OP.is_equal)
+    run("v", V.memset, [], ["xf"], T.xf[:, 32:33], -1.0)
+    run("v", V.memset, [], ["xf"], T.xf[:, 65:66], -1.0)
+    vcopy(["xt"], ["xf"], T.xf[:, 0:32], T.xt[:, 0:32])
+    vcopy(["xt"], ["xf"], T.xf[:, 33:65], T.xt[:, 32:64])
+    ts(["gm", "pf"], ["b8"], T.b8[:, :], T.gm[:, :], T.col[:, 3:4], OP.is_equal)
+    ts(["gm", "pgf"], ["gf"], T.gf[:, :], T.gm[:, :], T.col[:, 2:3], OP.is_equal)
+    ts(["dj"], ["dk"], T.dk[:, :], T.dj[:, 0:256], 127, OP.bitwise_and)
+    ts(["dk"], ["i2b"], T.i2b[:, :], T.dk[:, :], 0.0, OP.is_equal)
+    ts(["xt", "rc"], ["xr"], T.xr[:, 32:128], T.xt[:, 32:128], T.col[:, 5:6], OP.add)
+    ts(["xr"], ["xr2"], T.xo[:, 32:128], T.xr[:, 32:128], 2047, OP.bitwise_and)
+    ts(["xr2"], ["xh"], T.xh[:, 64:128], T.xo[:, 64:128], 8, OP.logical_shift_right)
+    ts(["xh"], ["xh2"], T.xr[:, 64:96], T.xh[:, 64:96], 256.0, OP.mult)
+    ts(["xh"], ["xh2"], T.xr[:, 96:128], T.xh[:, 96:128], 256.0, OP.mult, 256.0, OP.add)
+    tt(["xr2", "xh2"], ["xh3"], T.xh[:, 64:128], T.xo[:, 64:128], T.xr[:, 64:128], OP.add)
+    vcopy(["xh3"], ["xucd"], T.xu[:, 64:128], T.xh[:, 64:128])
+    vcopy(["xr2"], ["xub"], T.xu[:, 32:64], T.xo[:, 32:64])
+    vcopy(["obt"], ["obu"], T.obu[:, :], T.obt[:, :])
+    ts(["jt", "g16"], ["jf"], T.jf[:, :], T.jt[:, :], T.col[:, 4:5], OP.subtract)
+    ts(["dj", "nz"], ["sh1"], T.sh1[:, :], T.dj[:, 0:128], 127.0, OP.is_equal, T.col[:, 0:1], OP.mult)
+    ts(["dj", "zf"], ["sh2"], T.sh2[:, :], T.dj[:, 0:128], 143.0, OP.is_equal, T.col[:, 1:2], OP.mult)
+    ts(["dk"], ["i2f"], T.i2f[:, :], T.dk[:, :], 0.0, OP.is_equal)
+
+    mm(["b8", "vin"], ["ps4"], bank(4)[:, :], T.b8[0:8, :], T.vin[0:8, :])
+    scopy(["ps4"], ["vr"], T.vr[:, :], bank(4)[:, :])
+    for i in range(16):
+        run("s", S.activation, ["xf", "d16"], ["y1"], T.y1[:, i::16], T.xf[:, :], AF.Copy, scale=T.d16[:, i:i + 1])
+    mm(["gf", "y1"], ["ps5"], bank(5)[:, :], T.gf[:, :], T.y1[:, 0:512])
+    scopy(["ps5"], ["fla"], T.fla[:, :], bank(5)[:, :])
+    mm(["gf", "y1"], ["ps6"], bank(6)[:, :], T.gf[:, :], T.y1[:, 528:1040])
+    scopy(["ps6"], ["flb"], T.flb[:, :], bank(6)[:, :])
+
+    def scatter_places(xkey, x, b, outkey, out):
+        k = "ps%d" % b
+        before("p", [xkey, "sh1", "sh2"], [k])
+        run("p", P.matmul, [xkey, "sh1"], [k], bank(b)[:, 0:32], T.sh1[:, :], x[:, 0:32], True, False)
+        run("p", P.matmul, [xkey, "sh2"], [k], bank(b)[:, 0:32], T.sh2[:, :], x[:, 1:33], False, True)
+        tt([xkey, k], [outkey + "e"], T.sa1[:, :], x[:, 0:32], bank(b)[:, 0:32], OP.not_equal)
+        tt([xkey, "jf"], [outkey + "d"], T.sa2[:, :], x[:, 0:32], T.jf[:, :], OP.subtract)
+        tt([outkey + "e", outkey + "d"], [outkey + "f"], T.sa2[:, :], T.sa2[:, :], T.sa1[:, :], OP.mult)
+        tt([outkey + "f", "jf"], [outkey + "h"], T.sa1[:, :], T.sa2[:, :], T.jf[:, :], OP.add)
+        vcopy([outkey + "h"], [outkey], out[:, :], T.sa1[:, :])
+
+    scatter_places("xf", T.xf, 7, "sau", T.sau)
+    run("v", V.memset, [], ["ma"], T.ma[:, 0:1], 0.0)
+    tt(["fla"], ["ma"], T.ma[:, 1:512], T.fla[:, 1:512], T.fla[:, 0:511], OP.is_equal)
+    run("v", V.memset, [], ["P1"], T.P1[:, 0:2048], 0.0)
+    scopy(["flb", "obu"], ["fbp"], T.fbp[:, :], T.flb[:, :].indirect(T.obu[:, :]))
+
+    def table(x, t, w, ident, ikey, banks, other, vec):
+        land, key = T["land" + x], "land" + x
+        dma("y", "cmp" + x, [key], [x + "0"], t[:, 0:w], land[:, :])
+        for d in range(4, 8):
+            q = other if d >= 6 else "y"
+            dma(q, "rot" + x, [key], ["%s%d" % (x, d)], t[0:128 - 16 * d, d * w:(d + 1) * w], land[128 * d:1024, :])
+            dma(q, "rot" + x, [key], ["%s%d" % (x, d)], t[128 - 16 * d:128, d * w:(d + 1) * w], land[0:128 * d, :])
+        for d in range(1, 4):
+            b = banks[d - 1]
+            mm([ikey, x + "0"], ["ps%d" % b], bank(b)[:, 0:w], ident[:, 16 * d:16 * d + 128], t[:, 0:w])
+            (vcopy if d in vec else scopy)(["ps%d" % b], ["%s%d" % (x, d)], t[:, d * w:(d + 1) * w], bank(b)[:, 0:w])
+        return ["%s%d" % (x, d) for d in range(8)]
+
+    kcd = table("cd", T.tcd, 512, T.i2b, "i2b", (0, 1, 2), "s", (2,))
+    kb = table("b", T.tb, 256, T.i2b, "i2b", (3, 4, 5), "y", ())
+    for k in range(8):
+        dma("y", "lda", [], ["fra"], T.fra[16 * k:16 * k + 16, :], T.fa[:, :])
+    tt(kcd + ["xucd", "vr"], ["w1"], T.w1[:, :], T.tcd[:, :].indirect(T.xu[:, 64:96]), T.vr[:, :], OP.mult)
+    tt(kcd + ["xucd", "w1"], ["w2"], T.w2[:, :], T.tcd[:, :].indirect(T.xu[:, 96:128]), T.w1[:, :], OP.mult)
+    tt(kb + ["xub", "w2"], ["pr1"], T.pr1[:, :], T.tb[:, :].indirect(T.xu[:, 32:64]), T.w2[:, :], OP.mult)
+    scopy(["w2", "obu"], ["wp"], T.wp[:, :], T.w2[:, :].indirect(T.obu[:, :]))
+
+    def segsum(mkey, m, pkey, p, skey, s, ukey, u, zkey, z):
+        run("v", V.tensor_tensor_scan, [mkey, pkey], [skey], s[:, :], m[:, :], p[:, :], 0.0, OP.mult, OP.add)
+        vcopy([skey, ukey, zkey], [zkey + "s"], z[:, :].indirect(u[:, :]), s[:, :])
+
+    def reduce(keys, z, x, u, r, vec):
+        for h in range(2):
+            b = 6 + h
+            for q in range(8):
+                c = 256 * q + 128 * h
+                mm(keys + ["d16"], ["ps%d" % b], bank(b)[:, 16 * q:16 * q + 16], z[:, c:c + 128], T.d16[:, 0:16])
+            (vcopy if vec and h else scopy)(["ps%d" % b], ["%su%d" % (x, h)], u[:, 128 * h:128 * h + 128], bank(b)[:, 0:128])
+        for h in range(2):
+            b = 4 + h
+            run("p", P.transpose, ["%su%d" % (x, h), "i2f"], ["ps%d" % b], bank(b)[:, 0:128], u[:, 128 * h:128 * h + 128], T.i2f[:, 0:128])
+            (vcopy if vec and h else scopy)(["ps%d" % b], ["%sr%d" % (x, h)], r[:, 128 * h:128 * h + 128], bank(b)[:, 0:128])
+        return [x + "r0", x + "r1"]
+
+    segsum("ma", T.ma, "pr1", T.pr1, "sg1", T.sg1, "sau", T.sau, "P1", T.P1)
+    exchange("p1", T.r1, reduce(["P1", "P1s"], T.P1, "p1", T.u1, T.r1, False))
+
+    run("v", V.memset, [], ["mb"], T.mb[:, 0:1], 0.0)
+    tt(["fbp"], ["mb"], T.mb[:, 1:512], T.fbp[:, 1:512], T.fbp[:, 0:511], OP.is_equal)
+    tt(["flb", "obu", "d16"], ["ba"], T.ba[:, 0:512], T.flb[:, :].indirect(T.obu[:, :]), T.d16[:, :], OP.mult)
+    tt(["fla", "obu", "d16"], ["ba"], T.ba[:, 512:1024], T.fla[:, :].indirect(T.obu[:, :]), T.d16[:, :], OP.mult)
+    tt(["ba"], ["t1"], T.t1[:, :], T.ba[:, 0::2], T.ba[:, 1::2], OP.add)
+    tt(["t1"], ["t2"], T.t2[:, :], T.t1[:, 0::2], T.t1[:, 1::2], OP.add)
+    tt(["t2"], ["t3"], T.t3[:, :], T.t2[:, 0::2], T.t2[:, 1::2], OP.add)
+    tt(["t3"], ["t4"], T.t4[:, :], T.t3[:, 0::2], T.t3[:, 1::2], OP.add)
+    run("v", V.memset, [], ["xg"], T.xg[:, 32:33], -1.0)
+    vcopy(["t4"], ["xg"], T.xg[:, 0:32], T.t4[:, 0:32])
+    ts(["t4", "rc"], ["ai"], T.ai[:, :], T.t4[:, 32:64], T.col[:, 5:6], OP.add)
+    ts(["ai"], ["aj"], T.aj[:, :], T.ai[:, :], 2047, OP.bitwise_and)
+    vcopy(["aj"], ["au"], T.au[:, :], T.aj[:, :])
+    scatter_places("xg", T.xg, 3, "sbu", T.sbu)
+
+    dma("y", "lp1s", ["landp1"], ["lp1"], T.lp1[:, :], T.landp1[:, :])
+    vcopy(["lp1", "lu2", "Z1"], ["Z1s"], T.Z1[:, :].indirect(T.lu[:, 48:64]), T.lp1[:, :])
+    for k in range(4):
+        c = slice(512 * k, 512 * k + 512)
+        mm(["d16", "Z1", "Z1s"], ["ps%d" % k], bank(k)[:, :], T.d16[:, 0:128], T.Z1[:, c])
+        tt(["ps%d" % k, "fra"], ["yar"], T.yar[:, c], bank(k)[:, :], T.fra[:, c], OP.mult)
+    vcopy(["yar", "lu2"], ["ga"], T.ga[:, :], T.yar[:, :].indirect(T.lu[:, 48:64]))
+    exchange("a", T.ga, ["ga"])
+    run("g", g.iota, [], ["Z2"], T.Z2[:, :], [[0, 2048]], 0, 0, allow_small_or_imprecise_dtypes=True)
+    dma("y", "oya", ["yar"], [], T.ya[:, :], T.yar[0:16, :])
+
+    ka = table("a", T.ta, 256, T.i2f, "i2f", (0, 1, 2), "s", (2,))
+    tt(ka + ["au", "wp"], ["pr2"], T.pr2[:, :], T.ta[:, :].indirect(T.au[:, :]), T.wp[:, :], OP.mult)
+    segsum("mb", T.mb, "pr2", T.pr2, "sg2", T.sg2, "sbu", T.sbu, "P2", T.P2)
+    exchange("p2", T.r2, reduce(["P2", "P2s"], T.P2, "p2", T.u2, T.r2, True))
+
+    dma("y", "lp2s", ["landp2"], ["lp2"], T.lp2[:, :], T.landp2[:, :])
+    vcopy(["lp2", "lu2", "Z2"], ["Z2s"], T.Z2[:, :].indirect(T.lu[:, 32:48]), T.lp2[:, :])
+    kr = reduce(["Z2", "Z2s"], T.Z2, "yb", T.u3, T.r3, True)
+    for q in range(8):
+        dma("s" if q % 2 else "y", "oyb", kr, [], T.yb[:, 256 * q:256 * q + 256], T.r3[16 * q:16 * q + 16, :])
+
+    need("g", [(s, cnt[s]) for s in cnt])

@@ -3,16 +3,16 @@ from concourse.mybir import AluOpType as OP, ActivationFunctionType as AF
 
 F, B, I, U = "float32", "bfloat16", "int32", "uint16"
 SCRATCH = {
-    "din": ("sbuf", [128, 2048], B), "frc": ("sbuf", [128, 2048], B), "frd": ("sbuf", [128, 2048], B),
-    "frb": ("sbuf", [128, 2048], B), "fra": ("sbuf", [128, 2048], B),
+    "din": ("sbuf", [128, 2048], B), "bin": ("sbuf", [128, 2048], B), "frc": ("sbuf", [128, 2048], B),
+    "frd": ("sbuf", [128, 2048], B), "frb": ("sbuf", [128, 2048], B), "fra": ("sbuf", [128, 2048], B),
     "lt": ("sbuf", [128, 64], I), "lu": ("sbuf", [128, 64], U),
     "xt": ("sbuf", [128, 128], I), "xr": ("sbuf", [128, 128], I), "xh": ("sbuf", [128, 128], I),
     "xo": ("sbuf", [128, 128], I), "xu": ("sbuf", [128, 128], U),
     "obt": ("sbuf", [128, 32], I), "obu": ("sbuf", [128, 32], U),
     "vin": ("sbuf", [128, 512], F), "vr": ("sbuf", [128, 512], F),
-    "pc": ("sbuf", [128, 8], I), "dj": ("sbuf", [128, 512], I), "gm": ("sbuf", [128, 128], I), "jt": ("sbuf", [128, 32], I),
+    "pc": ("sbuf", [128, 8], I), "dj": ("sbuf", [128, 256], I), "gm": ("sbuf", [128, 128], I), "jt": ("sbuf", [128, 32], I),
     "pi": ("sbuf", [128, 8], I), "pg": ("sbuf", [128, 8], I), "col": ("sbuf", [128, 8], F),
-    "di": ("sbuf", [128, 512], I), "dk": ("sbuf", [128, 256], I), "d16": ("sbuf", [128, 512], F),
+    "di": ("sbuf", [128, 128], I), "dk": ("sbuf", [128, 256], I), "d16": ("sbuf", [128, 512], F),
     "eb": ("sbuf", [128, 128], B), "i2f": ("sbuf", [128, 256], F), "i2b": ("sbuf", [128, 256], B),
     "sh1": ("sbuf", [128, 128], F), "sh2": ("sbuf", [128, 128], F), "b8": ("sbuf", [128, 128], F),
     "gf": ("sbuf", [128, 128], F), "jf": ("sbuf", [128, 32], F),
@@ -132,31 +132,46 @@ def rank_program(g, core, T, topo):
 
     dma("y", "ldd", [], ["din"], T.din[0:16, :], T.fd[:, :])
     dma("y", "ldl1", [], ["lt1"], T.lt[:, 0:16], T.lc[:, :])
-    dma("y", "ldl1", [], ["lt1"], T.lt[:, 16:32], T.ld[:, :])
+    dma("s", "ldl1", [], ["lt1"], T.lt[:, 16:32], T.ld[:, :])
     for k in range(8):
         dma("s" if k % 2 else "y", "ldc", [], ["frc"], T.frc[16 * k:16 * k + 16, :], T.fc[:, :])
+    dma("y", "ldb", [], ["bin"], T.bin[0:16, :], T.fb[:, :])
     dma("s", "ldl2", [], ["lt2"], T.lt[:, 32:48], T.lb[:, :])
-    dma("y", "ldl2", [], ["lt2"], T.lt[:, 48:64], T.la[:, :])
-    for k in range(8):
-        dma("s" if k % 2 else "y", "ldb", [], ["frb"], T.frb[16 * k:16 * k + 16, :], T.fb[:, :])
+    dma("s", "ldl2", [], ["lt2"], T.lt[:, 48:64], T.la[:, :])
     dma("y", "ldv", [], ["vin"], T.vin[0:8, :], T.v[:, :])
     for k, x in enumerate((T.xa, T.xb, T.xc, T.xd)):
         dma("s" if k % 2 else "y", "ldx", [], ["xt"], T.xt[:, 32 * k:32 * k + 32], x[:, :])
     dma("y", "ldo", [], ["obt"], T.obt[:, :], T.ob[:, :])
 
-    run("g", g.iota, [], ["dj"], T.dj[:, :], [[1, 512]], 128, -1)
+    run("g", g.iota, [], ["dj"], T.dj[:, :], [[1, 256]], 128, -1)
     run("g", g.iota, [], ["pc"], T.pc[:, 0:1], [[1, 1]], 0, 1)
     run("g", g.iota, [], ["gm"], T.gm[:, :], [[1, 8], [0, 16]], 0, 0)
     run("g", g.iota, [], ["jt"], T.jt[:, :], [[16, 32]], 2048, 1)
-
-    ts(["dj"], ["di"], T.di[:, :], T.dj[:, :], 15, OP.bitwise_and)
-    ts(["di"], ["eb"], T.eb[:, :], T.di[:, 0:128], 0.0, OP.is_equal)
+    ts(["dj"], ["di"], T.di[:, :], T.dj[:, 0:128], 15, OP.bitwise_and)
+    ts(["di"], ["eb"], T.eb[:, :], T.di[:, :], 0.0, OP.is_equal)
+    ts(["di"], ["d16"], T.d16[:, 0:128], T.di[:, :], 0.0, OP.is_equal)
+    ts(["pc"], ["pi"], T.pi[:, 0:1], T.pc[:, 0:1], 15, OP.bitwise_and)
+    ts(["pc"], ["pg"], T.pg[:, 0:1], T.pc[:, 0:1], 4, OP.logical_shift_right)
+    vcopy(["pg"], ["pgf"], T.col[:, 2:3], T.pg[:, 0:1])
+    vcopy(["pc"], ["pf"], T.col[:, 3:4], T.pc[:, 0:1])
     vcopy(["lt1"], ["lu1"], T.lu[:, 0:32], T.lt[:, 0:32])
-    for k in range(4):
-        mm(["eb", "din"], ["ps%d" % k], bank(k)[:, :], T.eb[0:16, :], T.din[0:16, 512 * k:512 * k + 512])
-        (scopy if k % 2 == 0 else vcopy)(["ps%d" % k], ["frd%d" % k], T.frd[:, 512 * k:512 * k + 512], bank(k)[:, :])
-    scopy(["frd%d" % k for k in range(4)] + ["lu1"], ["gcdD"], T.gcd[:, 256:512], T.frd[:, :].indirect(T.lu[:, 16:32]))
+
+    def spread(src, skey, dst, dkey):
+        for k in range(4):
+            mm(["eb", skey], ["ps%d" % k], bank(k)[:, :], T.eb[0:16, :], src[0:16, 512 * k:512 * k + 512])
+            (scopy if k % 2 == 0 else vcopy)(["ps%d" % k], ["%s%d" % (dkey, k)], dst[:, 512 * k:512 * k + 512], bank(k)[:, :])
+        return ["%s%d" % (dkey, k) for k in range(4)]
+
+    kd = spread(T.din, "din", T.frd, "frd")
+    scopy(kd + ["lu1"], ["gcdD"], T.gcd[:, 256:512], T.frd[:, :].indirect(T.lu[:, 16:32]))
+    ts(["gm", "pf"], ["b8"], T.b8[:, :], T.gm[:, :], T.col[:, 3:4], OP.is_equal)
     vcopy(["frc", "lu1"], ["gcdC"], T.gcd[:, 0:256], T.frc[:, :].indirect(T.lu[:, 0:16]))
+    kbi = spread(T.bin, "bin", T.frb, "frb")
+    mm(["b8", "vin"], ["ps6"], bank(6)[:, :], T.b8[0:8, :], T.vin[0:8, :])
+    run("v", V.memset, [], ["xf"], T.xf[:, 32:33], -1.0)
+    run("v", V.memset, [], ["xf"], T.xf[:, 65:66], -1.0)
+    vcopy(["xt"], ["xf"], T.xf[:, 0:32], T.xt[:, 0:32])
+    vcopy(["xt"], ["xf"], T.xf[:, 33:65], T.xt[:, 32:64])
 
     plans = {c: send_engines(c, cores, topo) for c in cores}
 
@@ -181,28 +196,33 @@ def rank_program(g, core, T, topo):
 
     exchange("cd", T.gcd, ["gcdC", "gcdD"])
     vcopy(["lt2"], ["lu2"], T.lu[:, 32:64], T.lt[:, 32:64])
-    vcopy(["frb", "lu2"], ["gb"], T.gb[:, :], T.frb[:, :].indirect(T.lu[:, 32:48]))
+    vcopy(kbi + ["lu2"], ["gb"], T.gb[:, :], T.frb[:, :].indirect(T.lu[:, 32:48]))
     exchange("b", T.gb, ["gb"])
-    for z in ("Z1", "P2"):
+
+    def zeros(z):
         run("g", g.iota, [], [z], T[z][:, 0:2048], [[0, 2048]], 0, 0, allow_small_or_imprecise_dtypes=True)
 
-    ts(["pc"], ["pi"], T.pi[:, 0:1], T.pc[:, 0:1], 15, OP.bitwise_and)
-    ts(["pc"], ["pg"], T.pg[:, 0:1], T.pc[:, 0:1], 4, OP.logical_shift_right)
+    zeros("P1")
+    zeros("Z1")
+
+    for i in range(16):
+        if i % 2:
+            run("s", S.activation, ["xf", "d16"], ["y1s"], T.y1[:, i::16], T.xf[:, :], AF.Copy, scale=T.d16[:, i:i + 1])
+        else:
+            ts(["xf", "d16"], ["y1v"], T.y1[:, i::16], T.xf[:, :], T.d16[:, i:i + 1], OP.mult)
+    ts(["gm", "pgf"], ["gf"], T.gf[:, :], T.gm[:, :], T.col[:, 2:3], OP.is_equal)
+    mm(["gf", "y1s", "y1v"], ["ps5"], bank(5)[:, :], T.gf[:, :], T.y1[:, 0:512])
+    scopy(["ps6"], ["vr"], T.vr[:, :], bank(6)[:, :])
+    scopy(["ps5"], ["fla"], T.fla[:, :], bank(5)[:, :])
+    ts(["dj"], ["dk"], T.dk[:, :], T.dj[:, :], 127, OP.bitwise_and)
+    ts(["dk"], ["i2b"], T.i2b[:, :], T.dk[:, :], 0.0, OP.is_equal)
     ts(["pi"], ["nz"], T.col[:, 0:1], T.pi[:, 0:1], 0.0, OP.not_equal)
     ts(["pi"], ["zf"], T.col[:, 1:2], T.pi[:, 0:1], 0.0, OP.is_equal)
-    vcopy(["pg"], ["pgf"], T.col[:, 2:3], T.pg[:, 0:1])
-    vcopy(["pc"], ["pf"], T.col[:, 3:4], T.pc[:, 0:1])
     ts(["pg"], ["g16"], T.col[:, 4:5], T.pg[:, 0:1], 16.0, OP.mult)
     ts(["pg"], ["rc"], T.col[:, 5:6], T.pg[:, 0:1], -256.0, OP.mult, 2048.0, OP.add)
-    ts(["di"], ["d16"], T.d16[:, :], T.di[:, :], 0.0, OP.is_equal)
-    run("v", V.memset, [], ["xf"], T.xf[:, 32:33], -1.0)
-    run("v", V.memset, [], ["xf"], T.xf[:, 65:66], -1.0)
-    vcopy(["xt"], ["xf"], T.xf[:, 0:32], T.xt[:, 0:32])
-    vcopy(["xt"], ["xf"], T.xf[:, 33:65], T.xt[:, 32:64])
-    ts(["gm", "pf"], ["b8"], T.b8[:, :], T.gm[:, :], T.col[:, 3:4], OP.is_equal)
-    ts(["gm", "pgf"], ["gf"], T.gf[:, :], T.gm[:, :], T.col[:, 2:3], OP.is_equal)
-    ts(["dj"], ["dk"], T.dk[:, :], T.dj[:, 0:256], 127, OP.bitwise_and)
-    ts(["dk"], ["i2b"], T.i2b[:, :], T.dk[:, :], 0.0, OP.is_equal)
+    ts(["jt", "g16"], ["jf"], T.jf[:, :], T.jt[:, :], T.col[:, 4:5], OP.subtract)
+    ts(["dj", "nz"], ["sh1"], T.sh1[:, :], T.dj[:, 0:128], 127.0, OP.is_equal, T.col[:, 0:1], OP.mult)
+    ts(["dj", "zf"], ["sh2"], T.sh2[:, :], T.dj[:, 0:128], 143.0, OP.is_equal, T.col[:, 1:2], OP.mult)
     ts(["xt", "rc"], ["xr"], T.xr[:, 32:128], T.xt[:, 32:128], T.col[:, 5:6], OP.add)
     ts(["xr"], ["xr2"], T.xo[:, 32:128], T.xr[:, 32:128], 2047, OP.bitwise_and)
     ts(["xr2"], ["xh"], T.xh[:, 64:128], T.xo[:, 64:128], 8, OP.logical_shift_right)
@@ -211,20 +231,6 @@ def rank_program(g, core, T, topo):
     tt(["xr2", "xh2"], ["xh3"], T.xh[:, 64:128], T.xo[:, 64:128], T.xr[:, 64:128], OP.add)
     vcopy(["xh3"], ["xucd"], T.xu[:, 64:128], T.xh[:, 64:128])
     vcopy(["xr2"], ["xub"], T.xu[:, 32:64], T.xo[:, 32:64])
-    vcopy(["obt"], ["obu"], T.obu[:, :], T.obt[:, :])
-    ts(["jt", "g16"], ["jf"], T.jf[:, :], T.jt[:, :], T.col[:, 4:5], OP.subtract)
-    ts(["dj", "nz"], ["sh1"], T.sh1[:, :], T.dj[:, 0:128], 127.0, OP.is_equal, T.col[:, 0:1], OP.mult)
-    ts(["dj", "zf"], ["sh2"], T.sh2[:, :], T.dj[:, 0:128], 143.0, OP.is_equal, T.col[:, 1:2], OP.mult)
-    ts(["dk"], ["i2f"], T.i2f[:, :], T.dk[:, :], 0.0, OP.is_equal)
-
-    mm(["b8", "vin"], ["ps4"], bank(4)[:, :], T.b8[0:8, :], T.vin[0:8, :])
-    scopy(["ps4"], ["vr"], T.vr[:, :], bank(4)[:, :])
-    for i in range(16):
-        run("s", S.activation, ["xf", "d16"], ["y1"], T.y1[:, i::16], T.xf[:, :], AF.Copy, scale=T.d16[:, i:i + 1])
-    mm(["gf", "y1"], ["ps5"], bank(5)[:, :], T.gf[:, :], T.y1[:, 0:512])
-    scopy(["ps5"], ["fla"], T.fla[:, :], bank(5)[:, :])
-    mm(["gf", "y1"], ["ps6"], bank(6)[:, :], T.gf[:, :], T.y1[:, 528:1040])
-    scopy(["ps6"], ["flb"], T.flb[:, :], bank(6)[:, :])
 
     def scatter_places(xkey, x, b, outkey, out):
         k = "ps%d" % b
@@ -239,31 +245,33 @@ def rank_program(g, core, T, topo):
 
     scatter_places("xf", T.xf, 7, "sau", T.sau)
     run("v", V.memset, [], ["ma"], T.ma[:, 0:1], 0.0)
-    tt(["fla"], ["ma"], T.ma[:, 1:512], T.fla[:, 1:512], T.fla[:, 0:511], OP.is_equal)
-    run("v", V.memset, [], ["P1"], T.P1[:, 0:2048], 0.0)
-    scopy(["flb", "obu"], ["fbp"], T.fbp[:, :], T.flb[:, :].indirect(T.obu[:, :]))
+    tt(["fla", "ps5"], ["ma"], T.ma[:, 1:512], T.fla[:, 1:512], bank(5)[:, 0:511], OP.is_equal)
+    vcopy(["obt"], ["obu"], T.obu[:, :], T.obt[:, :])
 
     def table(x, t, w, ident, ikey, banks, other, vec):
-        land, key = T["land" + x], "land" + x
+        land, key, n = T["land" + x], "land" + x, 1 + len(banks)
         dma("y", "cmp" + x, [key], [x + "0"], t[:, 0:w], land[:, :])
-        for d in range(4, 8):
-            q = other if d >= 6 else "y"
+        for d in range(n, 8):
+            q = other if d % 2 else "y"
             dma(q, "rot" + x, [key], ["%s%d" % (x, d)], t[0:128 - 16 * d, d * w:(d + 1) * w], land[128 * d:1024, :])
             dma(q, "rot" + x, [key], ["%s%d" % (x, d)], t[128 - 16 * d:128, d * w:(d + 1) * w], land[0:128 * d, :])
-        for d in range(1, 4):
+        for d in range(1, n):
             b = banks[d - 1]
             mm([ikey, x + "0"], ["ps%d" % b], bank(b)[:, 0:w], ident[:, 16 * d:16 * d + 128], t[:, 0:w])
             (vcopy if d in vec else scopy)(["ps%d" % b], ["%s%d" % (x, d)], t[:, d * w:(d + 1) * w], bank(b)[:, 0:w])
         return ["%s%d" % (x, d) for d in range(8)]
 
-    kcd = table("cd", T.tcd, 512, T.i2b, "i2b", (0, 1, 2), "s", (2,))
-    kb = table("b", T.tb, 256, T.i2b, "i2b", (3, 4, 5), "y", ())
-    for k in range(8):
-        dma("y", "lda", [], ["fra"], T.fra[16 * k:16 * k + 16, :], T.fa[:, :])
+    kcd = table("cd", T.tcd, 512, T.i2b, "i2b", (0, 1, 2, 3, 4), "y", (2, 4))
     tt(kcd + ["xucd", "vr"], ["w1"], T.w1[:, :], T.tcd[:, :].indirect(T.xu[:, 64:96]), T.vr[:, :], OP.mult)
     tt(kcd + ["xucd", "w1"], ["w2"], T.w2[:, :], T.tcd[:, :].indirect(T.xu[:, 96:128]), T.w1[:, :], OP.mult)
+    kb = table("b", T.tb, 256, T.i2b, "i2b", (5, 6, 7, 0, 1), "y", (2, 4))
+    for k in range(8):
+        dma("y", "lda", [], ["fra"], T.fra[16 * k:16 * k + 16, :], T.fa[:, :])
     tt(kb + ["xub", "w2"], ["pr1"], T.pr1[:, :], T.tb[:, :].indirect(T.xu[:, 32:64]), T.w2[:, :], OP.mult)
-    scopy(["w2", "obu"], ["wp"], T.wp[:, :], T.w2[:, :].indirect(T.obu[:, :]))
+    mm(["gf", "y1s", "y1v"], ["ps4"], bank(4)[:, :], T.gf[:, :], T.y1[:, 528:1040])
+    scopy(["ps4"], ["flb"], T.flb[:, :], bank(4)[:, :])
+    for k in range(1, 4):
+        scopy(["d16"], ["d16t"], T.d16[:, 128 * k:128 * k + 128], T.d16[:, 0:128])
 
     def segsum(mkey, m, pkey, p, skey, s, ukey, u, zkey, z):
         run("v", V.tensor_tensor_scan, [mkey, pkey], [skey], s[:, :], m[:, :], p[:, :], 0.0, OP.mult, OP.add)
@@ -283,12 +291,14 @@ def rank_program(g, core, T, topo):
         return [x + "r0", x + "r1"]
 
     segsum("ma", T.ma, "pr1", T.pr1, "sg1", T.sg1, "sau", T.sau, "P1", T.P1)
+    ts(["dk"], ["i2f"], T.i2f[:, :], T.dk[:, :], 0.0, OP.is_equal)
     exchange("p1", T.r1, reduce(["P1", "P1s"], T.P1, "p1", T.u1, T.r1, False))
+    zeros("P2")
 
-    run("v", V.memset, [], ["mb"], T.mb[:, 0:1], 0.0)
-    tt(["fbp"], ["mb"], T.mb[:, 1:512], T.fbp[:, 1:512], T.fbp[:, 0:511], OP.is_equal)
-    tt(["flb", "obu", "d16"], ["ba"], T.ba[:, 0:512], T.flb[:, :].indirect(T.obu[:, :]), T.d16[:, :], OP.mult)
-    tt(["fla", "obu", "d16"], ["ba"], T.ba[:, 512:1024], T.fla[:, :].indirect(T.obu[:, :]), T.d16[:, :], OP.mult)
+    scopy(["flb", "obu"], ["fbp"], T.fbp[:, :], T.flb[:, :].indirect(T.obu[:, :]))
+    scopy(["w2", "obu"], ["wp"], T.wp[:, :], T.w2[:, :].indirect(T.obu[:, :]))
+    tt(["flb", "obu", "d16", "d16t"], ["ba"], T.ba[:, 0:512], T.flb[:, :].indirect(T.obu[:, :]), T.d16[:, :], OP.mult)
+    tt(["fla", "obu", "d16", "d16t"], ["ba"], T.ba[:, 512:1024], T.fla[:, :].indirect(T.obu[:, :]), T.d16[:, :], OP.mult)
     tt(["ba"], ["t1"], T.t1[:, :], T.ba[:, 0::2], T.ba[:, 1::2], OP.add)
     tt(["t1"], ["t2"], T.t2[:, :], T.t1[:, 0::2], T.t1[:, 1::2], OP.add)
     tt(["t2"], ["t3"], T.t3[:, :], T.t2[:, 0::2], T.t2[:, 1::2], OP.add)
@@ -299,16 +309,19 @@ def rank_program(g, core, T, topo):
     ts(["ai"], ["aj"], T.aj[:, :], T.ai[:, :], 2047, OP.bitwise_and)
     vcopy(["aj"], ["au"], T.au[:, :], T.aj[:, :])
     scatter_places("xg", T.xg, 3, "sbu", T.sbu)
+    run("v", V.memset, [], ["mb"], T.mb[:, 0:1], 0.0)
+    tt(["fbp"], ["mb"], T.mb[:, 1:512], T.fbp[:, 1:512], T.fbp[:, 0:511], OP.is_equal)
 
     dma("y", "lp1s", ["landp1"], ["lp1"], T.lp1[:, :], T.landp1[:, :])
     vcopy(["lp1", "lu2", "Z1"], ["Z1s"], T.Z1[:, :].indirect(T.lu[:, 48:64]), T.lp1[:, :])
-    for k in range(4):
-        c = slice(512 * k, 512 * k + 512)
-        mm(["d16", "Z1", "Z1s"], ["ps%d" % k], bank(k)[:, :], T.d16[:, 0:128], T.Z1[:, c])
-        tt(["ps%d" % k, "fra"], ["yar"], T.yar[:, c], bank(k)[:, :], T.fra[:, c], OP.mult)
-    vcopy(["yar", "lu2"], ["ga"], T.ga[:, :], T.yar[:, :].indirect(T.lu[:, 48:64]))
-    exchange("a", T.ga, ["ga"])
-    run("g", g.iota, [], ["Z2"], T.Z2[:, :], [[0, 2048]], 0, 0, allow_small_or_imprecise_dtypes=True)
+    for k, (c0, c1) in enumerate(((0, 512), (512, 1024), (1024, 1536), (1536, 1792), (1792, 2048))):
+        c = slice(c0, c1)
+        mm(["d16", "Z1", "Z1s"], ["ps%d" % k], bank(k)[:, 0:c1 - c0], T.d16[:, 0:128], T.Z1[:, c])
+        tt(["ps%d" % k, "fra"], ["yar"], T.yar[:, c], bank(k)[:, 0:c1 - c0], T.fra[:, c], OP.mult)
+    scopy(["yar", "lu2"], ["gaS"], T.ga[:, 128:256], T.yar[:, :].indirect(T.lu[:, 56:64]))
+    vcopy(["yar", "lu2"], ["gaV"], T.ga[:, 0:128], T.yar[:, :].indirect(T.lu[:, 48:56]))
+    exchange("a", T.ga, ["gaS", "gaV"])
+    zeros("Z2")
     dma("y", "oya", ["yar"], [], T.ya[:, :], T.yar[0:16, :])
 
     ka = table("a", T.ta, 256, T.i2f, "i2f", (0, 1, 2), "s", (2,))

@@ -6,13 +6,12 @@ SCRATCH = {
     "din": ("sbuf", [128, 2048], B), "bin": ("sbuf", [128, 2048], B), "frc": ("sbuf", [128, 2048], B),
     "frd": ("sbuf", [128, 2048], B), "frb": ("sbuf", [128, 2048], B), "fra": ("sbuf", [128, 2048], B),
     "lt": ("sbuf", [128, 64], I), "lu": ("sbuf", [128, 64], U),
-    "xt": ("sbuf", [128, 128], I), "xr": ("sbuf", [128, 128], I), "xh": ("sbuf", [128, 128], I),
-    "xo": ("sbuf", [128, 128], I), "xu": ("sbuf", [128, 128], U),
+    "xt": ("sbuf", [128, 128], I), "xr": ("sbuf", [128, 128], I), "xo": ("sbuf", [128, 128], I), "xu": ("sbuf", [128, 128], U),
     "obt": ("sbuf", [128, 32], I), "obu": ("sbuf", [128, 32], U),
     "vin": ("sbuf", [128, 512], F), "vr": ("sbuf", [128, 512], F),
     "pc": ("sbuf", [128, 8], I), "dj": ("sbuf", [128, 256], I), "gm": ("sbuf", [128, 128], I), "jt": ("sbuf", [128, 32], I),
     "pi": ("sbuf", [128, 8], I), "pg": ("sbuf", [128, 8], I), "col": ("sbuf", [128, 8], F),
-    "di": ("sbuf", [128, 128], I), "dk": ("sbuf", [128, 256], I), "d16": ("sbuf", [128, 512], F),
+    "di": ("sbuf", [128, 128], I), "dk": ("sbuf", [128, 256], I), "d16": ("sbuf", [128, 512], F), "e2": ("sbuf", [128, 64], F),
     "eb": ("sbuf", [128, 128], B), "i2f": ("sbuf", [128, 256], F), "i2b": ("sbuf", [128, 256], B),
     "sh1": ("sbuf", [128, 128], F), "sh2": ("sbuf", [128, 128], F), "b8": ("sbuf", [128, 128], F),
     "gf": ("sbuf", [128, 128], F), "jf": ("sbuf", [128, 32], F),
@@ -23,41 +22,55 @@ SCRATCH = {
     "ba": ("sbuf", [128, 1024], F), "t1": ("sbuf", [128, 512], F), "t2": ("sbuf", [128, 256], F),
     "t3": ("sbuf", [128, 128], F), "t4": ("sbuf", [128, 64], F), "xg": ("sbuf", [128, 40], F),
     "ai": ("sbuf", [128, 32], I), "aj": ("sbuf", [128, 32], I), "au": ("sbuf", [128, 32], U),
-    "gcd": ("sbuf", [128, 512], B), "gb": ("sbuf", [128, 256], B),
-    "sndcd": ("dram", [1024, 64], B), "landcd": ("dram", [1024, 64], B),
+    "gd": ("sbuf", [128, 256], B), "gk": ("sbuf", [128, 256], B), "gb": ("sbuf", [128, 256], B),
+    "sndd": ("dram", [1024, 32], B), "landd": ("dram", [1024, 32], B),
+    "sndc": ("dram", [1024, 32], B), "landc": ("dram", [1024, 32], B),
     "sndb": ("dram", [1024, 32], B), "landb": ("dram", [1024, 32], B),
-    "tcd": ("sbuf", [128, 4096], B), "tb": ("sbuf", [128, 2048], B), "ta": ("sbuf", [128, 2048], F),
+    "snda": ("dram", [1024, 32], F), "landa": ("dram", [1024, 32], F),
+    "td": ("sbuf", [128, 2048], B), "tc": ("sbuf", [128, 2048], B), "tb": ("sbuf", [128, 2048], B), "ta": ("sbuf", [128, 2048], F),
     "w1": ("sbuf", [128, 512], F), "w2": ("sbuf", [128, 512], F), "wp": ("sbuf", [128, 512], F),
     "pr1": ("sbuf", [128, 512], F), "pr2": ("sbuf", [128, 512], F), "sg1": ("sbuf", [128, 512], F), "sg2": ("sbuf", [128, 512], F),
     "P1": ("sbuf", [128, 2560], F), "P2": ("sbuf", [128, 2560], F), "Z1": ("sbuf", [128, 2048], F), "Z2": ("sbuf", [128, 2048], F),
-    "u1": ("sbuf", [128, 256], F), "u2": ("sbuf", [128, 256], F), "u3": ("sbuf", [128, 256], F),
-    "r1": ("sbuf", [128, 256], F), "r2": ("sbuf", [128, 256], F), "r3": ("sbuf", [128, 256], F),
-    "sndp1": ("dram", [1024, 32], F), "landp1": ("dram", [1024, 32], F), "lp1": ("sbuf", [128, 256], F),
-    "snda": ("dram", [1024, 32], F), "landa": ("dram", [1024, 32], F),
-    "sndp2": ("dram", [1024, 32], F), "landp2": ("dram", [1024, 32], F), "lp2": ("sbuf", [128, 256], F),
+    "r1": ("sbuf", [128, 256], F), "r2": ("sbuf", [128, 256], F), "u3": ("sbuf", [128, 256], F), "r3": ("sbuf", [128, 256], F),
+    "lp1": ("sbuf", [128, 256], F), "lq1": ("sbuf", [128, 256], F), "lp2": ("sbuf", [128, 256], F), "lq2": ("sbuf", [128, 256], F),
     "yar": ("sbuf", [128, 2048], F), "ga": ("sbuf", [128, 256], F),
     "ps0": ("psum", [128, 512], F), "ps1": ("psum", [128, 512], F), "ps2": ("psum", [128, 512], F), "ps3": ("psum", [128, 512], F),
     "ps4": ("psum", [128, 512], F), "ps5": ("psum", [128, 512], F), "ps6": ("psum", [128, 512], F), "ps7": ("psum", [128, 512], F),
 }
-EXCH = ["cd", "b", "p1", "a", "p2"]
-SEMAPHORES = (["c_g", "c_v", "c_s", "c_p", "ldd", "ldl1", "ldl2", "ldc", "ldb", "lda", "ldx", "ldo", "ldv", "oya", "oyb",
-               "lp1s", "lp2s"] + [k + x for x in EXCH for k in ("snd", "self", "arr", "loc")]
-              + [k + x for x in ("cd", "b", "a") for k in ("cmp", "rot")])
+EXCH = ["d", "c", "b", "a"]
+SEMAPHORES = (["c_g", "c_v", "c_s", "c_p", "ldd", "ldl1", "ldl2", "ldl3", "ldc", "ldb", "lda", "ldx", "ldo", "ldv", "oya", "oyb"]
+              + [k + x for x in EXCH for k in ("snd", "self", "arr", "loc", "cmp", "rot")]
+              + [k + x for x in ("p1", "p2") for k in ("arr", "loc")])
+
+
+def ways(src, cores, topo):
+    off = [d for d in cores if topo.chip(d) != topo.chip(src)]
+    on = [d for d in cores if d != src and topo.chip(d) == topo.chip(src)]
+    far = [d for d in off if not topo.mates(topo.chip(src), topo.chip(d)) and not topo.same_plane(topo.chip(src), topo.chip(d))]
+    return far, [d for d in off if d not in far], on
 
 
 def send_engines(src, cores, topo):
-    off = [d for d in cores if topo.chip(d) != topo.chip(src)]
-    on = [d for d in cores if d != src and topo.chip(d) == topo.chip(src)]
-    e = topo.engines(src, off[0])
-    far = [d for d in off if not topo.mates(topo.chip(src), topo.chip(d)) and not topo.same_plane(topo.chip(src), topo.chip(d))]
-    near = [d for d in off if d not in far]
+    far, near, on = ways(src, cores, topo)
+    e = topo.engines(src, near[0])
     one, two = e[0::2], e[1::2]
     n = len(two) // len(far)
     p = {d: [one[i]] for i, d in enumerate(near)}
     p.update({d: two[i * n:(i + 1) * n] for i, d in enumerate(far)})
-    for d in on:
-        p[d] = [x for x in topo.engines(src, d) if x not in e][0:4:2]
+    for i, d in enumerate(on):
+        p[d] = [x for x in topo.engines(src, d) if x not in e][i:i + 1]
     return p
+
+
+def sum_calls(src, cores, topo):
+    far, near, on = ways(src, cores, topo)
+    off = far + near
+    e = topo.engines(src, off[0])
+    n = len(e) // 2
+    calls = [[(off[2 * k], e[0:n]), (off[2 * k + 1], e[n:2 * n])] for k in range(len(off) // 2)]
+    for d in on:
+        calls[-1].append((d, [x for x in topo.engines(src, d) if x not in e][0:n]))
+    return calls
 
 
 def rank_program(g, core, T, topo):
@@ -131,22 +144,21 @@ def rank_program(g, core, T, topo):
         return T["ps%d" % i]
 
     dma("y", "ldd", [], ["din"], T.din[0:16, :], T.fd[:, :])
-    dma("y", "ldl1", [], ["lt1"], T.lt[:, 0:16], T.lc[:, :])
     dma("s", "ldl1", [], ["lt1"], T.lt[:, 16:32], T.ld[:, :])
+    dma("y", "ldl1", [], ["lt1"], T.lt[:, 0:16], T.lc[:, :])
     for k in range(8):
         dma("s" if k % 2 else "y", "ldc", [], ["frc"], T.frc[16 * k:16 * k + 16, :], T.fc[:, :])
     dma("y", "ldb", [], ["bin"], T.bin[0:16, :], T.fb[:, :])
     dma("s", "ldl2", [], ["lt2"], T.lt[:, 32:48], T.lb[:, :])
-    dma("s", "ldl2", [], ["lt2"], T.lt[:, 48:64], T.la[:, :])
-    dma("y", "ldv", [], ["vin"], T.vin[0:8, :], T.v[:, :])
-    for k, x in enumerate((T.xa, T.xb, T.xc, T.xd)):
-        dma("s" if k % 2 else "y", "ldx", [], ["xt"], T.xt[:, 32 * k:32 * k + 32], x[:, :])
-    dma("y", "ldo", [], ["obt"], T.obt[:, :], T.ob[:, :])
+
+    def zeros(z, c0, c1):
+        run("g", g.iota, [], [z], T[z][:, c0:c1], [[0, c1 - c0]], 0, 0, allow_small_or_imprecise_dtypes=True)
 
     run("g", g.iota, [], ["dj"], T.dj[:, :], [[1, 256]], 128, -1)
     run("g", g.iota, [], ["pc"], T.pc[:, 0:1], [[1, 1]], 0, 1)
     run("g", g.iota, [], ["gm"], T.gm[:, :], [[1, 8], [0, 16]], 0, 0)
     run("g", g.iota, [], ["jt"], T.jt[:, :], [[16, 32]], 2048, 1)
+    zeros("P1", 0, 1024)
     ts(["dj"], ["di"], T.di[:, :], T.dj[:, 0:128], 15, OP.bitwise_and)
     ts(["di"], ["eb"], T.eb[:, :], T.di[:, :], 0.0, OP.is_equal)
     ts(["di"], ["d16"], T.d16[:, 0:128], T.di[:, :], 0.0, OP.is_equal)
@@ -154,6 +166,9 @@ def rank_program(g, core, T, topo):
     ts(["pc"], ["pg"], T.pg[:, 0:1], T.pc[:, 0:1], 4, OP.logical_shift_right)
     vcopy(["pg"], ["pgf"], T.col[:, 2:3], T.pg[:, 0:1])
     vcopy(["pc"], ["pf"], T.col[:, 3:4], T.pc[:, 0:1])
+    run("v", V.memset, [], ["xf"], T.xf[:, 32:33], -1.0)
+    run("v", V.memset, [], ["xf"], T.xf[:, 65:66], -1.0)
+    ts(["gm", "pf"], ["b8"], T.b8[:, :], T.gm[:, :], T.col[:, 3:4], OP.is_equal)
     vcopy(["lt1"], ["lu1"], T.lu[:, 0:32], T.lt[:, 0:32])
 
     def spread(src, skey, dst, dkey):
@@ -162,75 +177,73 @@ def rank_program(g, core, T, topo):
             (scopy if k % 2 == 0 else vcopy)(["ps%d" % k], ["%s%d" % (dkey, k)], dst[:, 512 * k:512 * k + 512], bank(k)[:, :])
         return ["%s%d" % (dkey, k) for k in range(4)]
 
-    kd = spread(T.din, "din", T.frd, "frd")
-    scopy(kd + ["lu1"], ["gcdD"], T.gcd[:, 256:512], T.frd[:, :].indirect(T.lu[:, 16:32]))
-    ts(["gm", "pf"], ["b8"], T.b8[:, :], T.gm[:, :], T.col[:, 3:4], OP.is_equal)
-    vcopy(["frc", "lu1"], ["gcdC"], T.gcd[:, 0:256], T.frc[:, :].indirect(T.lu[:, 0:16]))
-    kbi = spread(T.bin, "bin", T.frb, "frb")
-    mm(["b8", "vin"], ["ps6"], bank(6)[:, :], T.b8[0:8, :], T.vin[0:8, :])
-    run("v", V.memset, [], ["xf"], T.xf[:, 32:33], -1.0)
-    run("v", V.memset, [], ["xf"], T.xf[:, 65:66], -1.0)
-    vcopy(["xt"], ["xf"], T.xf[:, 0:32], T.xt[:, 0:32])
-    vcopy(["xt"], ["xf"], T.xf[:, 33:65], T.xt[:, 32:64])
+    def pick(keys, out, okey, src, c):
+        scopy(keys, [okey + "S"], out[:, 0:128], src[:, :].indirect(T.lu[:, c:c + 8]))
+        vcopy(keys, [okey + "V"], out[:, 128:256], src[:, :].indirect(T.lu[:, c + 8:c + 16]))
+        return [okey + "S", okey + "V"]
 
     plans = {c: send_engines(c, cores, topo) for c in cores}
+
+    def transfer(src, dst, d, es, x):
+        rid, pid, _ = topo.addr(d)
+        mask = 0
+        for e in es:
+            mask |= 1 << e
+        return RemoteDMATransfer(dst_ids=[DstId(rid=rid, pnc=pid)], dma_engine_mask=mask, remote_sem=T.sem["arr" + x], src=src, dst=dst)
 
     def exchange(x, src, keys):
         snd, land = T["snd" + x], T["land" + x]
         dma("y", "snd" + x, keys, ["snd" + x], snd[:, :], src[:, :])
         dma("y", "self" + x, keys, ["land" + x], land[128 * me:128 * me + 128, :], src[16 * me:16 * me + 16, :])
         before("g", ["snd" + x], [])
-        tr = []
-        for d, es in plans[core].items():
-            r = cores.index(d)
-            rid, pid, _ = topo.addr(d)
-            mask = 0
-            for e in es:
-                mask |= 1 << e
-            tr.append(RemoteDMATransfer(dst_ids=[DstId(rid=rid, pnc=pid)], dma_engine_mask=mask, remote_sem=T.sem["arr" + x],
-                                        src=snd[128 * r:128 * r + 128, :], dst=land[128 * me:128 * me + 128, :]))
-        g.remote_dma_fused(tr, local_sem=T.sem["loc" + x])
+        g.remote_dma_fused([transfer(snd[128 * cores.index(d):128 * cores.index(d) + 128, :], land[128 * me:128 * me + 128, :], d, es, x)
+                            for d, es in plans[core].items()], local_sem=T.sem["loc" + x])
         cnt["loc" + x] = sum(len(es) for es in plans[core].values())
         cnt["arr" + x] = sum(len(plans[c][core]) for c in cores if c != core)
         after("remote", ("arr" + x, None), [], ["land" + x])
 
-    exchange("cd", T.gcd, ["gcdC", "gcdD"])
-    vcopy(["lt2"], ["lu2"], T.lu[:, 32:64], T.lt[:, 32:64])
-    vcopy(kbi + ["lu2"], ["gb"], T.gb[:, :], T.frb[:, :].indirect(T.lu[:, 32:48]))
-    exchange("b", T.gb, ["gb"])
+    kd = spread(T.din, "din", T.frd, "frd")
+    exchange("d", T.gd, pick(kd + ["lu1"], T.gd, "gd", T.frd, 16))
+    exchange("c", T.gk, pick(["frc", "lu1"], T.gk, "gk", T.frc, 0))
+    dma("y", "ldl3", [], ["lt3"], T.lt[:, 48:64], T.la[:, :])
+    dma("y", "ldv", [], ["vin"], T.vin[0:8, :], T.v[:, :])
+    for k, x in enumerate((T.xa, T.xb, T.xc, T.xd)):
+        dma("y", "ldx", [], ["xt"], T.xt[:, 32 * k:32 * k + 32], x[:, :])
+    dma("y", "ldo", [], ["obt"], T.obt[:, :], T.ob[:, :])
+    ts(["pi"], ["nz"], T.col[:, 0:1], T.pi[:, 0:1], 0.0, OP.not_equal)
+    ts(["pi"], ["zf"], T.col[:, 1:2], T.pi[:, 0:1], 0.0, OP.is_equal)
+    ts(["pg"], ["g16"], T.col[:, 4:5], T.pg[:, 0:1], 16.0, OP.mult)
+    ts(["pg"], ["rc"], T.col[:, 5:6], T.pg[:, 0:1], -256.0, OP.mult, 2048.0, OP.add)
+    kbi = spread(T.bin, "bin", T.frb, "frb")
+    vcopy(["lt2"], ["lu2"], T.lu[:, 32:48], T.lt[:, 32:48])
+    exchange("b", T.gb, pick(kbi + ["lu2"], T.gb, "gb", T.frb, 32))
+    mm(["b8", "vin"], ["ps6"], bank(6)[:, :], T.b8[0:8, :], T.vin[0:8, :])
+    zeros("P1", 1024, 2048)
+    zeros("Z1", 0, 2048)
 
-    def zeros(z):
-        run("g", g.iota, [], [z], T[z][:, 0:2048], [[0, 2048]], 0, 0, allow_small_or_imprecise_dtypes=True)
-
-    zeros("P1")
-    zeros("Z1")
-
+    ts(["dj"], ["dk"], T.dk[:, :], T.dj[:, :], 127, OP.bitwise_and)
+    ts(["dk"], ["i2b"], T.i2b[:, :], T.dk[:, :], 0.0, OP.is_equal)
+    ts(["gm", "pgf"], ["gf"], T.gf[:, :], T.gm[:, :], T.col[:, 2:3], OP.is_equal)
+    ts(["jt", "g16"], ["jf"], T.jf[:, :], T.jt[:, :], T.col[:, 4:5], OP.subtract)
+    ts(["dj", "nz"], ["sh1"], T.sh1[:, :], T.dj[:, 0:128], 127.0, OP.is_equal, T.col[:, 0:1], OP.mult)
+    ts(["dj", "zf"], ["sh2"], T.sh2[:, :], T.dj[:, 0:128], 143.0, OP.is_equal, T.col[:, 1:2], OP.mult)
+    run("v", V.memset, [], ["e2"], T.e2[:, :], 0.0)
+    vcopy(["d16", "e2"], ["e2a"], T.e2[:, 0:32:2], T.d16[:, 0:16])
+    vcopy(["d16", "e2"], ["e2b"], T.e2[:, 33:64:2], T.d16[:, 0:16])
+    ts(["xt", "rc"], ["xr"], T.xr[:, 32:128], T.xt[:, 32:128], T.col[:, 5:6], OP.add)
+    ts(["xr"], ["xo"], T.xo[:, 32:128], T.xr[:, 32:128], 2047, OP.bitwise_and)
+    vcopy(["xo"], ["xu"], T.xu[:, 32:128], T.xo[:, 32:128])
+    vcopy(["xt"], ["xf"], T.xf[:, 0:32], T.xt[:, 0:32])
+    vcopy(["xt"], ["xf"], T.xf[:, 33:65], T.xt[:, 32:64])
+    vcopy(["lt3"], ["lu3"], T.lu[:, 48:64], T.lt[:, 48:64])
+    scopy(["ps6"], ["vr"], T.vr[:, :], bank(6)[:, :])
     for i in range(16):
         if i % 2:
             run("s", S.activation, ["xf", "d16"], ["y1s"], T.y1[:, i::16], T.xf[:, :], AF.Copy, scale=T.d16[:, i:i + 1])
         else:
             ts(["xf", "d16"], ["y1v"], T.y1[:, i::16], T.xf[:, :], T.d16[:, i:i + 1], OP.mult)
-    ts(["gm", "pgf"], ["gf"], T.gf[:, :], T.gm[:, :], T.col[:, 2:3], OP.is_equal)
     mm(["gf", "y1s", "y1v"], ["ps5"], bank(5)[:, :], T.gf[:, :], T.y1[:, 0:512])
-    scopy(["ps6"], ["vr"], T.vr[:, :], bank(6)[:, :])
     scopy(["ps5"], ["fla"], T.fla[:, :], bank(5)[:, :])
-    ts(["dj"], ["dk"], T.dk[:, :], T.dj[:, :], 127, OP.bitwise_and)
-    ts(["dk"], ["i2b"], T.i2b[:, :], T.dk[:, :], 0.0, OP.is_equal)
-    ts(["pi"], ["nz"], T.col[:, 0:1], T.pi[:, 0:1], 0.0, OP.not_equal)
-    ts(["pi"], ["zf"], T.col[:, 1:2], T.pi[:, 0:1], 0.0, OP.is_equal)
-    ts(["pg"], ["g16"], T.col[:, 4:5], T.pg[:, 0:1], 16.0, OP.mult)
-    ts(["pg"], ["rc"], T.col[:, 5:6], T.pg[:, 0:1], -256.0, OP.mult, 2048.0, OP.add)
-    ts(["jt", "g16"], ["jf"], T.jf[:, :], T.jt[:, :], T.col[:, 4:5], OP.subtract)
-    ts(["dj", "nz"], ["sh1"], T.sh1[:, :], T.dj[:, 0:128], 127.0, OP.is_equal, T.col[:, 0:1], OP.mult)
-    ts(["dj", "zf"], ["sh2"], T.sh2[:, :], T.dj[:, 0:128], 143.0, OP.is_equal, T.col[:, 1:2], OP.mult)
-    ts(["xt", "rc"], ["xr"], T.xr[:, 32:128], T.xt[:, 32:128], T.col[:, 5:6], OP.add)
-    ts(["xr"], ["xr2"], T.xo[:, 32:128], T.xr[:, 32:128], 2047, OP.bitwise_and)
-    ts(["xr2"], ["xh"], T.xh[:, 64:128], T.xo[:, 64:128], 8, OP.logical_shift_right)
-    ts(["xh"], ["xh2"], T.xr[:, 64:96], T.xh[:, 64:96], 256.0, OP.mult)
-    ts(["xh"], ["xh2"], T.xr[:, 96:128], T.xh[:, 96:128], 256.0, OP.mult, 256.0, OP.add)
-    tt(["xr2", "xh2"], ["xh3"], T.xh[:, 64:128], T.xo[:, 64:128], T.xr[:, 64:128], OP.add)
-    vcopy(["xh3"], ["xucd"], T.xu[:, 64:128], T.xh[:, 64:128])
-    vcopy(["xr2"], ["xub"], T.xu[:, 32:64], T.xo[:, 32:64])
 
     def scatter_places(xkey, x, b, outkey, out):
         k = "ps%d" % b
@@ -246,60 +259,95 @@ def rank_program(g, core, T, topo):
     scatter_places("xf", T.xf, 7, "sau", T.sau)
     run("v", V.memset, [], ["ma"], T.ma[:, 0:1], 0.0)
     tt(["fla", "ps5"], ["ma"], T.ma[:, 1:512], T.fla[:, 1:512], bank(5)[:, 0:511], OP.is_equal)
-    vcopy(["obt"], ["obu"], T.obu[:, :], T.obt[:, :])
 
-    def table(x, t, w, ident, ikey, banks, other, vec):
-        land, key, n = T["land" + x], "land" + x, 1 + len(banks)
+    def table(x, t, ident, ikey, groups, queues):
+        land, key, w = T["land" + x], "land" + x, 256
         dma("y", "cmp" + x, [key], [x + "0"], t[:, 0:w], land[:, :])
-        for d in range(n, 8):
-            q = other if d % 2 else "y"
-            dma(q, "rot" + x, [key], ["%s%d" % (x, d)], t[0:128 - 16 * d, d * w:(d + 1) * w], land[128 * d:1024, :])
-            dma(q, "rot" + x, [key], ["%s%d" % (x, d)], t[128 - 16 * d:128, d * w:(d + 1) * w], land[0:128 * d, :])
-        for d in range(1, n):
-            b = banks[d - 1]
-            mm([ikey, x + "0"], ["ps%d" % b], bank(b)[:, 0:w], ident[:, 16 * d:16 * d + 128], t[:, 0:w])
-            (vcopy if d in vec else scopy)(["ps%d" % b], ["%s%d" % (x, d)], t[:, d * w:(d + 1) * w], bank(b)[:, 0:w])
+        byp = [d for _, ds, _ in groups for d in ds]
+        for d in range(1, 8):
+            if d not in byp:
+                q = queues[d % len(queues)]
+                dma(q, "rot" + x, [key], ["%s%d" % (x, d)], t[0:128 - 16 * d, d * w:(d + 1) * w], land[128 * d:1024, :])
+                dma(q, "rot" + x, [key], ["%s%d" % (x, d)], t[128 - 16 * d:128, d * w:(d + 1) * w], land[0:128 * d, :])
+        for b, ds, q in groups:
+            n = len(ds)
+            for i, d in enumerate(ds):
+                mm([ikey, x + "0"], ["ps%d" % b], bank(b)[:, i * w:(i + 1) * w], ident[:, 16 * d:16 * d + 128], t[:, 0:w])
+            (vcopy if q == "v" else scopy)(["ps%d" % b], ["%s%d" % (x, d) for d in ds], t[:, ds[0] * w:(ds[0] + n) * w], bank(b)[:, 0:n * w])
         return ["%s%d" % (x, d) for d in range(8)]
 
-    kcd = table("cd", T.tcd, 512, T.i2b, "i2b", (0, 1, 2, 3, 4), "y", (2, 4))
-    tt(kcd + ["xucd", "vr"], ["w1"], T.w1[:, :], T.tcd[:, :].indirect(T.xu[:, 64:96]), T.vr[:, :], OP.mult)
-    tt(kcd + ["xucd", "w1"], ["w2"], T.w2[:, :], T.tcd[:, :].indirect(T.xu[:, 96:128]), T.w1[:, :], OP.mult)
-    kb = table("b", T.tb, 256, T.i2b, "i2b", (5, 6, 7, 0, 1), "y", (2, 4))
+    kd = table("d", T.td, T.i2b, "i2b", ((0, (1, 2), "s"), (1, (3, 4), "v"), (2, (5,), "s"), (4, (6,), "v")), "y")
+    tt(kd + ["xu", "vr"], ["w1"], T.w1[:, :], T.td[:, :].indirect(T.xu[:, 96:128]), T.vr[:, :], OP.mult)
+    kc = table("c", T.tc, T.i2b, "i2b", ((3, (1, 2), "s"), (7, (3, 4), "s"), (6, (5,), "v")), "y")
+    tt(kc + ["xu", "w1"], ["w2"], T.w2[:, :], T.tc[:, :].indirect(T.xu[:, 64:96]), T.w1[:, :], OP.mult)
+    kb = table("b", T.tb, T.i2b, "i2b", ((0, (1, 2), "s"), (1, (3, 4), "s")), "y")
     for k in range(8):
         dma("y", "lda", [], ["fra"], T.fra[16 * k:16 * k + 16, :], T.fa[:, :])
-    tt(kb + ["xub", "w2"], ["pr1"], T.pr1[:, :], T.tb[:, :].indirect(T.xu[:, 32:64]), T.w2[:, :], OP.mult)
+    tt(kb + ["xu", "w2"], ["pr1"], T.pr1[:, :], T.tb[:, :].indirect(T.xu[:, 32:64]), T.w2[:, :], OP.mult)
     mm(["gf", "y1s", "y1v"], ["ps4"], bank(4)[:, :], T.gf[:, :], T.y1[:, 528:1040])
     scopy(["ps4"], ["flb"], T.flb[:, :], bank(4)[:, :])
     for k in range(1, 4):
         scopy(["d16"], ["d16t"], T.d16[:, 128 * k:128 * k + 128], T.d16[:, 0:128])
+    vcopy(["obt"], ["obu"], T.obu[:, :], T.obt[:, :])
 
     def segsum(mkey, m, pkey, p, skey, s, ukey, u, zkey, z):
         run("v", V.tensor_tensor_scan, [mkey, pkey], [skey], s[:, :], m[:, :], p[:, :], 0.0, OP.mult, OP.add)
         vcopy([skey, ukey, zkey], [zkey + "s"], z[:, :].indirect(u[:, :]), s[:, :])
 
-    def reduce(keys, z, x, u, r, vec):
+    calls = {c: sum_calls(c, cores, topo) for c in cores}
+
+    def sums_out(x, keys, z, r, lp):
+        def add(q, b, c):
+            for h in range(2):
+                run("p", P.matmul, keys + ["d16", "e2a", "e2b"], ["ps%d" % b], bank(b)[:, c:c + 32],
+                    z[:, 256 * q + 128 * h:256 * q + 128 * h + 128], T.e2[:, 32 * h:32 * h + 32], h == 0, h == 1)
+        pos = 0
+        for k, call in enumerate(calls[core]):
+            n = 32 * len(call)
+            for j, (d, _) in enumerate(call):
+                add(cores.index(d), k, 32 * j)
+            (vcopy if k % 2 else scopy)(["ps%d" % k], ["%sr%d" % (x, k)], r[:, pos:pos + n], bank(k)[:, 0:n])
+            before("g", ["%sr%d" % (x, k)], [])
+            g.remote_dma_fused([transfer(r[:, pos + 32 * j:pos + 32 * j + 32], lp[:, 32 * me:32 * me + 32], d, es, x)
+                                for j, (d, es) in enumerate(call)], local_sem=T.sem["loc" + x])
+            pos += n
+        add(me, 4, 0)
+        vcopy(["ps4"], [x + "me"], lp[:, 32 * me:32 * me + 32], bank(4)[:, 0:32])
+        cnt["loc" + x] = sum(len(es) for call in calls[core] for _, es in call)
+        cnt["arr" + x] = sum(len(es) for c in cores if c != core for call in calls[c] for d, es in call if d == core)
+        after("remote", ("arr" + x, None), [], ["land" + x])
+
+    def sums_in(x, lp, lq, c, zkey, z):
         for h in range(2):
-            b = 6 + h
-            for q in range(8):
-                c = 256 * q + 128 * h
-                mm(keys + ["d16"], ["ps%d" % b], bank(b)[:, 16 * q:16 * q + 16], z[:, c:c + 128], T.d16[:, 0:16])
-            (vcopy if vec and h else scopy)(["ps%d" % b], ["%su%d" % (x, h)], u[:, 128 * h:128 * h + 128], bank(b)[:, 0:128])
+            mm(["land" + x, x + "me", "i2f"], ["ps%d" % (5 + h)], bank(5 + h)[:, 0:128], lp[:, h::2], T.i2f[:, 0:128])
+            scopy(["ps%d" % (5 + h)], ["%st%d" % (x, h)], lq[:, 128 * h:128 * h + 128], bank(5 + h)[:, 0:128])
         for h in range(2):
-            b = 4 + h
-            run("p", P.transpose, ["%su%d" % (x, h), "i2f"], ["ps%d" % b], bank(b)[:, 0:128], u[:, 128 * h:128 * h + 128], T.i2f[:, 0:128])
-            (vcopy if vec and h else scopy)(["ps%d" % b], ["%sr%d" % (x, h)], r[:, 128 * h:128 * h + 128], bank(b)[:, 0:128])
-        return [x + "r0", x + "r1"]
+            vcopy(["%st%d" % (x, h), "lu2", "lu3", zkey] + [zkey + "s0"] * h, ["%ss%d" % (zkey, h)],
+                  z[:, :].indirect(T.lu[:, c + 8 * h:c + 8 * h + 8]), lq[:, 128 * h:128 * h + 128])
+        return [zkey, zkey + "s0", zkey + "s1"]
 
     segsum("ma", T.ma, "pr1", T.pr1, "sg1", T.sg1, "sau", T.sau, "P1", T.P1)
+    sums_out("p1", ["P1", "P1s"], T.P1, T.r1, T.lp1)
     ts(["dk"], ["i2f"], T.i2f[:, :], T.dk[:, :], 0.0, OP.is_equal)
-    exchange("p1", T.r1, reduce(["P1", "P1s"], T.P1, "p1", T.u1, T.r1, False))
-    zeros("P2")
+    zeros("P2", 0, 2048)
 
     scopy(["flb", "obu"], ["fbp"], T.fbp[:, :], T.flb[:, :].indirect(T.obu[:, :]))
     scopy(["w2", "obu"], ["wp"], T.wp[:, :], T.w2[:, :].indirect(T.obu[:, :]))
     tt(["flb", "obu", "d16", "d16t"], ["ba"], T.ba[:, 0:512], T.flb[:, :].indirect(T.obu[:, :]), T.d16[:, :], OP.mult)
     tt(["fla", "obu", "d16", "d16t"], ["ba"], T.ba[:, 512:1024], T.fla[:, :].indirect(T.obu[:, :]), T.d16[:, :], OP.mult)
     tt(["ba"], ["t1"], T.t1[:, :], T.ba[:, 0::2], T.ba[:, 1::2], OP.add)
+
+    kz = sums_in("p1", T.lp1, T.lq1, 48, "Z1", T.Z1)
+    for k, (c0, c1) in enumerate(((0, 512), (512, 1024), (1024, 1536), (1536, 1792), (1792, 2048))):
+        c = slice(c0, c1)
+        mm(["d16"] + kz, ["ps%d" % k], bank(k)[:, 0:c1 - c0], T.d16[:, 0:128], T.Z1[:, c])
+        tt(["ps%d" % k, "fra"], ["yar"], T.yar[:, c], bank(k)[:, 0:c1 - c0], T.fra[:, c], OP.mult)
+    scopy(["yar", "lu3"], ["gaS"], T.ga[:, 128:256], T.yar[:, :].indirect(T.lu[:, 56:64]))
+    vcopy(["yar", "lu3"], ["gaV"], T.ga[:, 0:128], T.yar[:, :].indirect(T.lu[:, 48:56]))
+    exchange("a", T.ga, ["gaS", "gaV"])
+    zeros("Z2", 0, 2048)
+    dma("y", "oya", ["yar"], [], T.ya[:, :], T.yar[0:16, :])
+
     tt(["t1"], ["t2"], T.t2[:, :], T.t1[:, 0::2], T.t1[:, 1::2], OP.add)
     tt(["t2"], ["t3"], T.t3[:, :], T.t2[:, 0::2], T.t2[:, 1::2], OP.add)
     tt(["t3"], ["t4"], T.t4[:, :], T.t3[:, 0::2], T.t3[:, 1::2], OP.add)
@@ -308,30 +356,26 @@ def rank_program(g, core, T, topo):
     ts(["t4", "rc"], ["ai"], T.ai[:, :], T.t4[:, 32:64], T.col[:, 5:6], OP.add)
     ts(["ai"], ["aj"], T.aj[:, :], T.ai[:, :], 2047, OP.bitwise_and)
     vcopy(["aj"], ["au"], T.au[:, :], T.aj[:, :])
-    scatter_places("xg", T.xg, 3, "sbu", T.sbu)
+    scatter_places("xg", T.xg, 7, "sbu", T.sbu)
     run("v", V.memset, [], ["mb"], T.mb[:, 0:1], 0.0)
     tt(["fbp"], ["mb"], T.mb[:, 1:512], T.fbp[:, 1:512], T.fbp[:, 0:511], OP.is_equal)
 
-    dma("y", "lp1s", ["landp1"], ["lp1"], T.lp1[:, :], T.landp1[:, :])
-    vcopy(["lp1", "lu2", "Z1"], ["Z1s"], T.Z1[:, :].indirect(T.lu[:, 48:64]), T.lp1[:, :])
-    for k, (c0, c1) in enumerate(((0, 512), (512, 1024), (1024, 1536), (1536, 1792), (1792, 2048))):
-        c = slice(c0, c1)
-        mm(["d16", "Z1", "Z1s"], ["ps%d" % k], bank(k)[:, 0:c1 - c0], T.d16[:, 0:128], T.Z1[:, c])
-        tt(["ps%d" % k, "fra"], ["yar"], T.yar[:, c], bank(k)[:, 0:c1 - c0], T.fra[:, c], OP.mult)
-    scopy(["yar", "lu2"], ["gaS"], T.ga[:, 128:256], T.yar[:, :].indirect(T.lu[:, 56:64]))
-    vcopy(["yar", "lu2"], ["gaV"], T.ga[:, 0:128], T.yar[:, :].indirect(T.lu[:, 48:56]))
-    exchange("a", T.ga, ["gaS", "gaV"])
-    zeros("Z2")
-    dma("y", "oya", ["yar"], [], T.ya[:, :], T.yar[0:16, :])
-
-    ka = table("a", T.ta, 256, T.i2f, "i2f", (0, 1, 2), "s", (2,))
+    ka = table("a", T.ta, T.i2f, "i2f", ((0, (1,), "s"), (1, (2,), "v"), (2, (3,), "s")), "y")
     tt(ka + ["au", "wp"], ["pr2"], T.pr2[:, :], T.ta[:, :].indirect(T.au[:, :]), T.wp[:, :], OP.mult)
     segsum("mb", T.mb, "pr2", T.pr2, "sg2", T.sg2, "sbu", T.sbu, "P2", T.P2)
-    exchange("p2", T.r2, reduce(["P2", "P2s"], T.P2, "p2", T.u2, T.r2, True))
+    sums_out("p2", ["P2", "P2s"], T.P2, T.r2, T.lp2)
 
-    dma("y", "lp2s", ["landp2"], ["lp2"], T.lp2[:, :], T.landp2[:, :])
-    vcopy(["lp2", "lu2", "Z2"], ["Z2s"], T.Z2[:, :].indirect(T.lu[:, 32:48]), T.lp2[:, :])
-    kr = reduce(["Z2", "Z2s"], T.Z2, "yb", T.u3, T.r3, True)
+    kz = sums_in("p2", T.lp2, T.lq2, 32, "Z2", T.Z2)
+    kr = []
+    for h in range(2):
+        for q in range(8):
+            c = 256 * q + 128 * h
+            mm(kz + ["d16"], ["ps%d" % h], bank(h)[:, 16 * q:16 * q + 16], T.Z2[:, c:c + 128], T.d16[:, 0:16])
+        (vcopy if h else scopy)(["ps%d" % h], ["u3%d" % h], T.u3[:, 128 * h:128 * h + 128], bank(h)[:, 0:128])
+    for h in range(2):
+        run("p", P.transpose, ["u3%d" % h, "i2f"], ["ps%d" % (2 + h)], bank(2 + h)[:, 0:128], T.u3[:, 128 * h:128 * h + 128], T.i2f[:, 0:128])
+        (vcopy if h else scopy)(["ps%d" % (2 + h)], ["r3%d" % h], T.r3[:, 128 * h:128 * h + 128], bank(2 + h)[:, 0:128])
+        kr.append("r3%d" % h)
     for q in range(8):
         dma("s" if q % 2 else "y", "oyb", kr, [], T.yb[:, 256 * q:256 * q + 256], T.r3[16 * q:16 * q + 16, :])
 

from concourse.bass import DstId, RemoteDMATransfer
from concourse.mybir import AluOpType as OP, ActivationFunctionType as AF

F, B, I, U = "float32", "bfloat16", "int32", "uint16"
SCRATCH = {
    "din": ("sbuf", [128, 2048], B), "bin": ("sbuf", [128, 2048], B), "frc": ("sbuf", [128, 2048], B),
    "frd": ("sbuf", [128, 2048], B), "frb": ("sbuf", [128, 2048], B), "fra": ("sbuf", [128, 2048], B),
    "lt": ("sbuf", [128, 64], I), "lu": ("sbuf", [128, 64], U),
    "xt": ("sbuf", [128, 128], I), "xr": ("sbuf", [128, 128], I), "xo": ("sbuf", [128, 128], I), "xu": ("sbuf", [128, 128], U),
    "obt": ("sbuf", [128, 32], I), "obu": ("sbuf", [128, 32], U),
    "vin": ("sbuf", [128, 512], F), "vr": ("sbuf", [128, 512], F),
    "pc": ("sbuf", [128, 8], I), "dj": ("sbuf", [128, 256], I), "gm": ("sbuf", [128, 128], I), "jt": ("sbuf", [128, 32], I),
    "pi": ("sbuf", [128, 8], I), "pg": ("sbuf", [128, 8], I), "col": ("sbuf", [128, 8], F),
    "di": ("sbuf", [128, 128], I), "dk": ("sbuf", [128, 256], I), "d16": ("sbuf", [128, 512], F), "e2": ("sbuf", [128, 64], F),
    "eb": ("sbuf", [128, 128], B), "i2f": ("sbuf", [128, 256], F), "i2b": ("sbuf", [128, 256], B),
    "sh1": ("sbuf", [128, 128], F), "sh2": ("sbuf", [128, 128], F), "b8": ("sbuf", [128, 128], F),
    "gf": ("sbuf", [128, 128], F), "jf": ("sbuf", [128, 32], F),
    "xf": ("sbuf", [128, 66], F), "y1": ("sbuf", [128, 1056], F), "fla": ("sbuf", [128, 512], F),
    "flb": ("sbuf", [128, 512], F), "fbp": ("sbuf", [128, 512], F),
    "ma": ("sbuf", [128, 512], F), "mb": ("sbuf", [128, 512], F),
    "sa1": ("sbuf", [128, 32], F), "sa2": ("sbuf", [128, 32], F), "sau": ("sbuf", [128, 32], U), "sbu": ("sbuf", [128, 32], U),
    "ba": ("sbuf", [128, 1024], F), "t1": ("sbuf", [128, 512], F), "t2": ("sbuf", [128, 256], F),
    "t3": ("sbuf", [128, 128], F), "t4": ("sbuf", [128, 64], F), "xg": ("sbuf", [128, 40], F),
    "ai": ("sbuf", [128, 32], I), "aj": ("sbuf", [128, 32], I), "au": ("sbuf", [128, 32], U),
    "gd": ("sbuf", [128, 256], B), "gk": ("sbuf", [128, 256], B), "gb": ("sbuf", [128, 256], B),
    "sndd": ("dram", [1024, 32], B), "landd": ("dram", [1024, 32], B),
    "sndc": ("dram", [1024, 32], B), "landc": ("dram", [1024, 32], B),
    "sndb": ("dram", [1024, 32], B), "landb": ("dram", [1024, 32], B),
    "snda": ("dram", [1024, 32], F), "landa": ("dram", [1024, 32], F),
    "td": ("sbuf", [128, 2048], B), "tc": ("sbuf", [128, 2048], B), "tb": ("sbuf", [128, 2048], B), "ta": ("sbuf", [128, 2048], F),
    "w1": ("sbuf", [128, 512], F), "w2": ("sbuf", [128, 512], F), "wp": ("sbuf", [128, 512], F),
    "pr1": ("sbuf", [128, 512], F), "pr2": ("sbuf", [128, 512], F), "sg1": ("sbuf", [128, 512], F), "sg2": ("sbuf", [128, 512], F),
    "P1": ("sbuf", [128, 2560], F), "P2": ("sbuf", [128, 2560], F), "Z1": ("sbuf", [128, 2048], F), "Z2": ("sbuf", [128, 2048], F),
    "r1": ("sbuf", [128, 256], F), "r2": ("sbuf", [128, 256], F), "u3": ("sbuf", [128, 256], F), "r3": ("sbuf", [128, 256], F),
    "lp1": ("sbuf", [128, 256], F), "lq1": ("sbuf", [128, 256], F), "lp2": ("sbuf", [128, 256], F), "lq2": ("sbuf", [128, 256], F),
    "yar": ("sbuf", [128, 2048], F), "ga": ("sbuf", [128, 256], F),
    "ps0": ("psum", [128, 512], F), "ps1": ("psum", [128, 512], F), "ps2": ("psum", [128, 512], F), "ps3": ("psum", [128, 512], F),
    "ps4": ("psum", [128, 512], F), "ps5": ("psum", [128, 512], F), "ps6": ("psum", [128, 512], F), "ps7": ("psum", [128, 512], F),
}
EXCH = ["d", "c", "b", "a"]
SEMAPHORES = (["c_g", "c_v", "c_s", "c_p", "ldd", "ldl1", "ldl2", "ldl3", "ldc", "ldb", "lda", "ldx", "ldo", "ldv", "oya", "oyb"]
              + [k + x for x in EXCH for k in ("snd", "self", "arr", "loc", "cmp", "rot")]
              + [k + x for x in ("p1", "p2") for k in ("arr", "loc")])


def ways(src, cores, topo):
    off = [d for d in cores if topo.chip(d) != topo.chip(src)]
    on = [d for d in cores if d != src and topo.chip(d) == topo.chip(src)]
    far = [d for d in off if not topo.mates(topo.chip(src), topo.chip(d)) and not topo.same_plane(topo.chip(src), topo.chip(d))]
    return far, [d for d in off if d not in far], on


def send_engines(src, cores, topo):
    far, near, on = ways(src, cores, topo)
    e = topo.engines(src, near[0])
    one, two = e[0::2], e[1::2]
    n = len(two) // len(far)
    p = {d: [one[i]] for i, d in enumerate(near)}
    p.update({d: two[i * n:(i + 1) * n] for i, d in enumerate(far)})
    for i, d in enumerate(on):
        p[d] = [x for x in topo.engines(src, d) if x not in e][i:i + 1]
    return p


def sum_calls(src, cores, topo):
    far, near, on = ways(src, cores, topo)
    off = far + near
    e = topo.engines(src, off[0])
    n = len(e) // 2
    calls = [[(off[2 * k], e[0:n]), (off[2 * k + 1], e[n:2 * n])] for k in range(len(off) // 2)]
    for d in on:
        calls[-1].append((d, [x for x in topo.engines(src, d) if x not in e][0:n]))
    return calls


def rank_program(g, core, T, topo):
    me = T.rank_of(core)
    if me is None:
        return
    cores = list(T.cores)
    eng = {"g": g, "v": g.vector, "s": g.scalar, "p": g.tensor, "y": g.sync}
    seen = {q: {} for q in eng}
    cnt, WR, RD = {}, {}, {}

    def need(q, toks):
        m = {}
        for s, n in toks:
            n = cnt[s] if n is None else n
            m[s] = max(m.get(s, 0), n)
        for s in m:
            if seen[q].get(s, 0) < m[s]:
                eng[q].wait_ge(T.sem[s], m[s])
                seen[q][s] = m[s]

    def before(q, rd, wr, own=None):
        own = own or q
        toks = []
        for k in rd:
            toks += [t for _, t in WR.get(k, [])]
        for k in wr:
            toks += [t for o, t in WR.get(k, []) + RD.get(k, []) if o != own]
        need(q, toks)

    def after(o, tok, rd, wr):
        for k in rd:
            RD.setdefault(k, []).append((o, tok))
        for k in wr:
            WR.setdefault(k, []).append((o, tok))

    def run(q, fn, rd, wr, *a, **k):
        before(q, rd, wr)
        s = "c_" + q
        cnt[s] = cnt.get(s, 0) + 1
        fn(*a, **k).then_inc(T.sem[s], 1)
        after(q, (s, cnt[s]), rd, wr)

    def dma(q, sem, rd, wr, out, in_):
        before(q, rd, wr, "d" + sem)
        cnt[sem] = cnt.get(sem, 0) + 16
        eng[q].dma_start(out, in_).then_inc(T.sem[sem], 16)
        after("d" + sem, (sem, None), rd, wr)

    V, S, P = g.vector, g.scalar, g.tensor

    def ts(rd, wr, out, in0, s1, op0, s2=None, op1=None):
        if op1 is None:
            run("v", V.tensor_scalar, rd, wr, out, in0, s1, None, op0)
        else:
            run("v", V.tensor_scalar, rd, wr, out, in0, s1, s2, op0, op1)

    def tt(rd, wr, out, a, b, op):
        run("v", V.tensor_tensor, rd, wr, out, a, b, op)

    def vcopy(rd, wr, out, in_):
        run("v", V.tensor_copy, rd, wr, out, in_)

    def scopy(rd, wr, out, in_):
        run("s", S.activation, rd, wr, out, in_, AF.Copy)

    def mm(rd, wr, out, lhsT, rhs):
        run("p", P.matmul, rd, wr, out, lhsT, rhs, True, True)

    def bank(i):
        return T["ps%d" % i]

    dma("y", "ldd", [], ["din"], T.din[0:16, :], T.fd[:, :])
    dma("s", "ldl1", [], ["lt1"], T.lt[:, 16:32], T.ld[:, :])
    dma("y", "ldl1", [], ["lt1"], T.lt[:, 0:16], T.lc[:, :])
    for k in range(8):
        dma("s" if k % 2 else "y", "ldc", [], ["frc"], T.frc[16 * k:16 * k + 16, :], T.fc[:, :])
    dma("y", "ldb", [], ["bin"], T.bin[0:16, :], T.fb[:, :])
    dma("s", "ldl2", [], ["lt2"], T.lt[:, 32:48], T.lb[:, :])

    def zeros(z, c0, c1):
        run("g", g.iota, [], [z], T[z][:, c0:c1], [[0, c1 - c0]], 0, 0, allow_small_or_imprecise_dtypes=True)

    run("g", g.iota, [], ["dj"], T.dj[:, :], [[1, 256]], 128, -1)
    run("g", g.iota, [], ["pc"], T.pc[:, 0:1], [[1, 1]], 0, 1)
    run("g", g.iota, [], ["gm"], T.gm[:, :], [[1, 8], [0, 16]], 0, 0)
    run("g", g.iota, [], ["jt"], T.jt[:, :], [[16, 32]], 2048, 1)
    zeros("P1", 0, 1024)
    ts(["dj"], ["di"], T.di[:, :], T.dj[:, 0:128], 15, OP.bitwise_and)
    ts(["di"], ["eb"], T.eb[:, :], T.di[:, :], 0.0, OP.is_equal)
    ts(["di"], ["d16"], T.d16[:, 0:128], T.di[:, :], 0.0, OP.is_equal)
    ts(["pc"], ["pi"], T.pi[:, 0:1], T.pc[:, 0:1], 15, OP.bitwise_and)
    ts(["pc"], ["pg"], T.pg[:, 0:1], T.pc[:, 0:1], 4, OP.logical_shift_right)
    vcopy(["pg"], ["pgf"], T.col[:, 2:3], T.pg[:, 0:1])
    vcopy(["pc"], ["pf"], T.col[:, 3:4], T.pc[:, 0:1])
    run("v", V.memset, [], ["xf"], T.xf[:, 32:33], -1.0)
    run("v", V.memset, [], ["xf"], T.xf[:, 65:66], -1.0)
    ts(["gm", "pf"], ["b8"], T.b8[:, :], T.gm[:, :], T.col[:, 3:4], OP.is_equal)
    vcopy(["lt1"], ["lu1"], T.lu[:, 0:32], T.lt[:, 0:32])

    def spread(src, skey, dst, dkey):
        for k in range(4):
            mm(["eb", skey], ["ps%d" % k], bank(k)[:, :], T.eb[0:16, :], src[0:16, 512 * k:512 * k + 512])
            (scopy if k % 2 == 0 else vcopy)(["ps%d" % k], ["%s%d" % (dkey, k)], dst[:, 512 * k:512 * k + 512], bank(k)[:, :])
        return ["%s%d" % (dkey, k) for k in range(4)]

    def pick(keys, out, okey, src, c):
        scopy(keys, [okey + "S"], out[:, 0:128], src[:, :].indirect(T.lu[:, c:c + 8]))
        vcopy(keys, [okey + "V"], out[:, 128:256], src[:, :].indirect(T.lu[:, c + 8:c + 16]))
        return [okey + "S", okey + "V"]

    plans = {c: send_engines(c, cores, topo) for c in cores}

    def transfer(src, dst, d, es, x):
        rid, pid, _ = topo.addr(d)
        mask = 0
        for e in es:
            mask |= 1 << e
        return RemoteDMATransfer(dst_ids=[DstId(rid=rid, pnc=pid)], dma_engine_mask=mask, remote_sem=T.sem["arr" + x], src=src, dst=dst)

    def exchange(x, src, keys):
        snd, land = T["snd" + x], T["land" + x]
        dma("y", "snd" + x, keys, ["snd" + x], snd[:, :], src[:, :])
        dma("y", "self" + x, keys, ["land" + x], land[128 * me:128 * me + 128, :], src[16 * me:16 * me + 16, :])
        before("g", ["snd" + x], [])
        g.remote_dma_fused([transfer(snd[128 * cores.index(d):128 * cores.index(d) + 128, :], land[128 * me:128 * me + 128, :], d, es, x)
                            for d, es in plans[core].items()], local_sem=T.sem["loc" + x])
        cnt["loc" + x] = sum(len(es) for es in plans[core].values())
        cnt["arr" + x] = sum(len(plans[c][core]) for c in cores if c != core)
        after("remote", ("arr" + x, None), [], ["land" + x])

    kd = spread(T.din, "din", T.frd, "frd")
    exchange("d", T.gd, pick(kd + ["lu1"], T.gd, "gd", T.frd, 16))
    exchange("c", T.gk, pick(["frc", "lu1"], T.gk, "gk", T.frc, 0))
    dma("y", "ldl3", [], ["lt3"], T.lt[:, 48:64], T.la[:, :])
    dma("y", "ldv", [], ["vin"], T.vin[0:8, :], T.v[:, :])
    for k, x in enumerate((T.xa, T.xb, T.xc, T.xd)):
        dma("y", "ldx", [], ["xt"], T.xt[:, 32 * k:32 * k + 32], x[:, :])
    dma("y", "ldo", [], ["obt"], T.obt[:, :], T.ob[:, :])
    ts(["pi"], ["nz"], T.col[:, 0:1], T.pi[:, 0:1], 0.0, OP.not_equal)
    ts(["pi"], ["zf"], T.col[:, 1:2], T.pi[:, 0:1], 0.0, OP.is_equal)
    ts(["pg"], ["g16"], T.col[:, 4:5], T.pg[:, 0:1], 16.0, OP.mult)
    ts(["pg"], ["rc"], T.col[:, 5:6], T.pg[:, 0:1], -256.0, OP.mult, 2048.0, OP.add)
    kbi = spread(T.bin, "bin", T.frb, "frb")
    vcopy(["lt2"], ["lu2"], T.lu[:, 32:48], T.lt[:, 32:48])
    exchange("b", T.gb, pick(kbi + ["lu2"], T.gb, "gb", T.frb, 32))
    mm(["b8", "vin"], ["ps6"], bank(6)[:, :], T.b8[0:8, :], T.vin[0:8, :])
    zeros("P1", 1024, 2048)
    zeros("Z1", 0, 2048)

    ts(["dj"], ["dk"], T.dk[:, :], T.dj[:, :], 127, OP.bitwise_and)
    ts(["dk"], ["i2b"], T.i2b[:, :], T.dk[:, :], 0.0, OP.is_equal)
    ts(["gm", "pgf"], ["gf"], T.gf[:, :], T.gm[:, :], T.col[:, 2:3], OP.is_equal)
    ts(["jt", "g16"], ["jf"], T.jf[:, :], T.jt[:, :], T.col[:, 4:5], OP.subtract)
    ts(["dj", "nz"], ["sh1"], T.sh1[:, :], T.dj[:, 0:128], 127.0, OP.is_equal, T.col[:, 0:1], OP.mult)
    ts(["dj", "zf"], ["sh2"], T.sh2[:, :], T.dj[:, 0:128], 143.0, OP.is_equal, T.col[:, 1:2], OP.mult)
    run("v", V.memset, [], ["e2"], T.e2[:, :], 0.0)
    vcopy(["d16", "e2"], ["e2a"], T.e2[:, 0:32:2], T.d16[:, 0:16])
    vcopy(["d16", "e2"], ["e2b"], T.e2[:, 33:64:2], T.d16[:, 0:16])
    ts(["xt", "rc"], ["xr"], T.xr[:, 32:128], T.xt[:, 32:128], T.col[:, 5:6], OP.add)
    ts(["xr"], ["xo"], T.xo[:, 32:128], T.xr[:, 32:128], 2047, OP.bitwise_and)
    vcopy(["xo"], ["xu"], T.xu[:, 32:128], T.xo[:, 32:128])
    vcopy(["xt"], ["xf"], T.xf[:, 0:32], T.xt[:, 0:32])
    vcopy(["xt"], ["xf"], T.xf[:, 33:65], T.xt[:, 32:64])
    vcopy(["lt3"], ["lu3"], T.lu[:, 48:64], T.lt[:, 48:64])
    scopy(["ps6"], ["vr"], T.vr[:, :], bank(6)[:, :])
    for i in range(16):
        if i % 2:
            run("s", S.activation, ["xf", "d16"], ["y1s"], T.y1[:, i::16], T.xf[:, :], AF.Copy, scale=T.d16[:, i:i + 1])
        else:
            ts(["xf", "d16"], ["y1v"], T.y1[:, i::16], T.xf[:, :], T.d16[:, i:i + 1], OP.mult)
    mm(["gf", "y1s", "y1v"], ["ps5"], bank(5)[:, :], T.gf[:, :], T.y1[:, 0:512])
    scopy(["ps5"], ["fla"], T.fla[:, :], bank(5)[:, :])

    def scatter_places(xkey, x, b, outkey, out):
        k = "ps%d" % b
        before("p", [xkey, "sh1", "sh2"], [k])
        run("p", P.matmul, [xkey, "sh1"], [k], bank(b)[:, 0:32], T.sh1[:, :], x[:, 0:32], True, False)
        run("p", P.matmul, [xkey, "sh2"], [k], bank(b)[:, 0:32], T.sh2[:, :], x[:, 1:33], False, True)
        tt([xkey, k], [outkey + "e"], T.sa1[:, :], x[:, 0:32], bank(b)[:, 0:32], OP.not_equal)
        tt([xkey, "jf"], [outkey + "d"], T.sa2[:, :], x[:, 0:32], T.jf[:, :], OP.subtract)
        tt([outkey + "e", outkey + "d"], [outkey + "f"], T.sa2[:, :], T.sa2[:, :], T.sa1[:, :], OP.mult)
        tt([outkey + "f", "jf"], [outkey + "h"], T.sa1[:, :], T.sa2[:, :], T.jf[:, :], OP.add)
        vcopy([outkey + "h"], [outkey], out[:, :], T.sa1[:, :])

    scatter_places("xf", T.xf, 7, "sau", T.sau)
    run("v", V.memset, [], ["ma"], T.ma[:, 0:1], 0.0)
    tt(["fla", "ps5"], ["ma"], T.ma[:, 1:512], T.fla[:, 1:512], bank(5)[:, 0:511], OP.is_equal)

    def table(x, t, ident, ikey, groups, queues):
        land, key, w = T["land" + x], "land" + x, 256
        dma("y", "cmp" + x, [key], [x + "0"], t[:, 0:w], land[:, :])
        byp = [d for _, ds, _ in groups for d in ds]
        for d in range(1, 8):
            if d not in byp:
                q = queues[d % len(queues)]
                dma(q, "rot" + x, [key], ["%s%d" % (x, d)], t[0:128 - 16 * d, d * w:(d + 1) * w], land[128 * d:1024, :])
                dma(q, "rot" + x, [key], ["%s%d" % (x, d)], t[128 - 16 * d:128, d * w:(d + 1) * w], land[0:128 * d, :])
        for b, ds, q in groups:
            n = len(ds)
            for i, d in enumerate(ds):
                mm([ikey, x + "0"], ["ps%d" % b], bank(b)[:, i * w:(i + 1) * w], ident[:, 16 * d:16 * d + 128], t[:, 0:w])
            (vcopy if q == "v" else scopy)(["ps%d" % b], ["%s%d" % (x, d) for d in ds], t[:, ds[0] * w:(ds[0] + n) * w], bank(b)[:, 0:n * w])
        return ["%s%d" % (x, d) for d in range(8)]

    kd = table("d", T.td, T.i2b, "i2b", ((0, (1, 2), "s"), (1, (3, 4), "v"), (2, (5,), "s"), (4, (6,), "v")), "y")
    tt(kd + ["xu", "vr"], ["w1"], T.w1[:, :], T.td[:, :].indirect(T.xu[:, 96:128]), T.vr[:, :], OP.mult)
    kc = table("c", T.tc, T.i2b, "i2b", ((3, (1, 2), "s"), (7, (3, 4), "s"), (6, (5,), "v")), "y")
    tt(kc + ["xu", "w1"], ["w2"], T.w2[:, :], T.tc[:, :].indirect(T.xu[:, 64:96]), T.w1[:, :], OP.mult)
    kb = table("b", T.tb, T.i2b, "i2b", ((0, (1, 2), "s"), (1, (3, 4), "s")), "y")
    for k in range(8):
        dma("y", "lda", [], ["fra"], T.fra[16 * k:16 * k + 16, :], T.fa[:, :])
    tt(kb + ["xu", "w2"], ["pr1"], T.pr1[:, :], T.tb[:, :].indirect(T.xu[:, 32:64]), T.w2[:, :], OP.mult)
    mm(["gf", "y1s", "y1v"], ["ps4"], bank(4)[:, :], T.gf[:, :], T.y1[:, 528:1040])
    scopy(["ps4"], ["flb"], T.flb[:, :], bank(4)[:, :])
    for k in range(1, 4):
        scopy(["d16"], ["d16t"], T.d16[:, 128 * k:128 * k + 128], T.d16[:, 0:128])
    vcopy(["obt"], ["obu"], T.obu[:, :], T.obt[:, :])

    def segsum(mkey, m, pkey, p, skey, s, ukey, u, zkey, z):
        run("v", V.tensor_tensor_scan, [mkey, pkey], [skey], s[:, :], m[:, :], p[:, :], 0.0, OP.mult, OP.add)
        vcopy([skey, ukey, zkey], [zkey + "s"], z[:, :].indirect(u[:, :]), s[:, :])

    calls = {c: sum_calls(c, cores, topo) for c in cores}

    def sums_out(x, keys, z, r, lp):
        def add(q, b, c):
            for h in range(2):
                run("p", P.matmul, keys + ["d16", "e2a", "e2b"], ["ps%d" % b], bank(b)[:, c:c + 32],
                    z[:, 256 * q + 128 * h:256 * q + 128 * h + 128], T.e2[:, 32 * h:32 * h + 32], h == 0, h == 1)
        pos = 0
        for k, call in enumerate(calls[core]):
            n = 32 * len(call)
            for j, (d, _) in enumerate(call):
                add(cores.index(d), k, 32 * j)
            (vcopy if k % 2 else scopy)(["ps%d" % k], ["%sr%d" % (x, k)], r[:, pos:pos + n], bank(k)[:, 0:n])
            before("g", ["%sr%d" % (x, k)], [])
            g.remote_dma_fused([transfer(r[:, pos + 32 * j:pos + 32 * j + 32], lp[:, 32 * me:32 * me + 32], d, es, x)
                                for j, (d, es) in enumerate(call)], local_sem=T.sem["loc" + x])
            pos += n
        add(me, 4, 0)
        vcopy(["ps4"], [x + "me"], lp[:, 32 * me:32 * me + 32], bank(4)[:, 0:32])
        cnt["loc" + x] = sum(len(es) for call in calls[core] for _, es in call)
        cnt["arr" + x] = sum(len(es) for c in cores if c != core for call in calls[c] for d, es in call if d == core)
        after("remote", ("arr" + x, None), [], ["land" + x])

    def sums_in(x, lp, lq, c, zkey, z):
        for h in range(2):
            mm(["land" + x, x + "me", "i2f"], ["ps%d" % (5 + h)], bank(5 + h)[:, 0:128], lp[:, h::2], T.i2f[:, 0:128])
            scopy(["ps%d" % (5 + h)], ["%st%d" % (x, h)], lq[:, 128 * h:128 * h + 128], bank(5 + h)[:, 0:128])
        for h in range(2):
            vcopy(["%st%d" % (x, h), "lu2", "lu3", zkey] + [zkey + "s0"] * h, ["%ss%d" % (zkey, h)],
                  z[:, :].indirect(T.lu[:, c + 8 * h:c + 8 * h + 8]), lq[:, 128 * h:128 * h + 128])
        return [zkey, zkey + "s0", zkey + "s1"]

    segsum("ma", T.ma, "pr1", T.pr1, "sg1", T.sg1, "sau", T.sau, "P1", T.P1)
    sums_out("p1", ["P1", "P1s"], T.P1, T.r1, T.lp1)
    ts(["dk"], ["i2f"], T.i2f[:, :], T.dk[:, :], 0.0, OP.is_equal)
    zeros("P2", 0, 2048)

    scopy(["flb", "obu"], ["fbp"], T.fbp[:, :], T.flb[:, :].indirect(T.obu[:, :]))
    scopy(["w2", "obu"], ["wp"], T.wp[:, :], T.w2[:, :].indirect(T.obu[:, :]))
    tt(["flb", "obu", "d16", "d16t"], ["ba"], T.ba[:, 0:512], T.flb[:, :].indirect(T.obu[:, :]), T.d16[:, :], OP.mult)
    tt(["fla", "obu", "d16", "d16t"], ["ba"], T.ba[:, 512:1024], T.fla[:, :].indirect(T.obu[:, :]), T.d16[:, :], OP.mult)
    tt(["ba"], ["t1"], T.t1[:, :], T.ba[:, 0::2], T.ba[:, 1::2], OP.add)

    kz = sums_in("p1", T.lp1, T.lq1, 48, "Z1", T.Z1)
    for k, (c0, c1) in enumerate(((0, 512), (512, 1024), (1024, 1536), (1536, 1792), (1792, 2048))):
        c = slice(c0, c1)
        mm(["d16"] + kz, ["ps%d" % k], bank(k)[:, 0:c1 - c0], T.d16[:, 0:128], T.Z1[:, c])
        tt(["ps%d" % k, "fra"], ["yar"], T.yar[:, c], bank(k)[:, 0:c1 - c0], T.fra[:, c], OP.mult)
    scopy(["yar", "lu3"], ["gaS"], T.ga[:, 128:256], T.yar[:, :].indirect(T.lu[:, 56:64]))
    vcopy(["yar", "lu3"], ["gaV"], T.ga[:, 0:128], T.yar[:, :].indirect(T.lu[:, 48:56]))
    exchange("a", T.ga, ["gaS", "gaV"])
    zeros("Z2", 0, 2048)
    dma("y", "oya", ["yar"], [], T.ya[:, :], T.yar[0:16, :])

    tt(["t1"], ["t2"], T.t2[:, :], T.t1[:, 0::2], T.t1[:, 1::2], OP.add)
    tt(["t2"], ["t3"], T.t3[:, :], T.t2[:, 0::2], T.t2[:, 1::2], OP.add)
    tt(["t3"], ["t4"], T.t4[:, :], T.t3[:, 0::2], T.t3[:, 1::2], OP.add)
    run("v", V.memset, [], ["xg"], T.xg[:, 32:33], -1.0)
    vcopy(["t4"], ["xg"], T.xg[:, 0:32], T.t4[:, 0:32])
    ts(["t4", "rc"], ["ai"], T.ai[:, :], T.t4[:, 32:64], T.col[:, 5:6], OP.add)
    ts(["ai"], ["aj"], T.aj[:, :], T.ai[:, :], 2047, OP.bitwise_and)
    vcopy(["aj"], ["au"], T.au[:, :], T.aj[:, :])
    scatter_places("xg", T.xg, 7, "sbu", T.sbu)
    run("v", V.memset, [], ["mb"], T.mb[:, 0:1], 0.0)
    tt(["fbp"], ["mb"], T.mb[:, 1:512], T.fbp[:, 1:512], T.fbp[:, 0:511], OP.is_equal)

    ka = table("a", T.ta, T.i2f, "i2f", ((0, (1,), "s"), (1, (2,), "v"), (2, (3,), "s")), "y")
    tt(ka + ["au", "wp"], ["pr2"], T.pr2[:, :], T.ta[:, :].indirect(T.au[:, :]), T.wp[:, :], OP.mult)
    segsum("mb", T.mb, "pr2", T.pr2, "sg2", T.sg2, "sbu", T.sbu, "P2", T.P2)
    sums_out("p2", ["P2", "P2s"], T.P2, T.r2, T.lp2)

    kz = sums_in("p2", T.lp2, T.lq2, 32, "Z2", T.Z2)
    kr = []
    for h in range(2):
        for q in range(8):
            c = 256 * q + 128 * h
            mm(kz + ["d16"], ["ps%d" % h], bank(h)[:, 16 * q:16 * q + 16], T.Z2[:, c:c + 128], T.d16[:, 0:16])
        (vcopy if h else scopy)(["ps%d" % h], ["u3%d" % h], T.u3[:, 128 * h:128 * h + 128], bank(h)[:, 0:128])
    for h in range(2):
        run("p", P.transpose, ["u3%d" % h, "i2f"], ["ps%d" % (2 + h)], bank(2 + h)[:, 0:128], T.u3[:, 128 * h:128 * h + 128], T.i2f[:, 0:128])
        (vcopy if h else scopy)(["ps%d" % (2 + h)], ["r3%d" % h], T.r3[:, 128 * h:128 * h + 128], bank(2 + h)[:, 0:128])
        kr.append("r3%d" % h)
    for q in range(8):
        dma("s" if q % 2 else "y", "oyb", kr, [], T.yb[:, 256 * q:256 * q + 256], T.r3[16 * q:16 * q + 16, :])

    need("g", [(s, cnt[s]) for s in cnt])
